import numpy as np, ml_dtypes
CORES = [16,17,18,19,32,33,34,35]
N = 8
BF = ml_dtypes.bfloat16
def f(rng, *shape):
    return (rng.standard_normal(shape, dtype=np.float32) * np.exp2(rng.integers(-2, 3, shape[:-1] + (1,)))).astype(BF)
def wide(rng, *shape):
    v = f(rng, *shape).astype(np.float32); k = shape[:-2] + (1, shape[-1])
    return (v * np.exp2(rng.integers(-6, 7, k)) * (rng.random(k) > 0.0625)).astype(BF)
D, H, B, R = 64, 8, 1, 3
STEP = 2.0 ** -12
def pack(cs):
    a = np.asarray(cs).reshape(N, B, 8, 2).transpose(0, 2, 1, 3).reshape(N, 8, 1, 2 * B)
    return np.ascontiguousarray(np.repeat(a, 16, axis=2).reshape(N, 128, 2 * B)).astype(np.int32)
def stripes(v):
    return np.ascontiguousarray(v.reshape(16, N, H * D).transpose(1, 0, 2))
def pictures(v):
    return np.ascontiguousarray(v.transpose(1, 0, 2)).reshape(16, D * D)
def setup_inputs(rng):
    A = 8 * B * N; th = 2 * np.pi * (rng.permutation(A) + 0.8 * rng.random(A)) / A
    fac = np.exp2(rng.permutation(np.repeat(np.array([-4, -2, 0, 1]), 4))).astype(np.float32)
    x = np.abs(f(rng, N, 16, H * D).astype(np.float32))
    mu = (rng.random((N, 16, H * D)) * 0.06 * (rng.random((N, 16, H * D)) > 0.2)).astype(np.float32)
    counts = np.abs(f(rng, N, 128, B * D).astype(np.float32)) * np.float32(64) * np.tile(fac, 8)[:, None]
    return {"x": x, "mu": mu, "counts": counts, "ang": pack(np.stack([np.rint(256 * np.cos(th)), np.rint(256 * np.sin(th))], -1))}
def setup_inputs_axes(rng):
    d = setup_inputs(rng); A = 8 * B * N
    t = np.array([[256, 0], [0, 256], [-256, 0], [0, -256], [181, 181], [-181, 181], [181, -181], [-181, -181]])
    d["ang"] = pack(t[rng.permutation(np.arange(A) % 8)]); return d
def setup_inputs_pairs(rng):
    d = setup_inputs(rng); A = 8 * B * N; cs = rng.integers(-256, 257, (A, 2))
    cs[rng.permutation(A)[:8]] = np.array([[0, 0], [256, 256], [-256, 256], [256, -256], [-256, -256], [1, 0], [0, -1], [5, -9]])
    d["ang"] = pack(cs); return d
def setup_inputs_edges(rng):
    d = setup_inputs(rng); m = np.zeros((D, D), np.float32); m[[0, -1]] = 1; m[:, [0, -1]] = 1
    d["x"] = stripes((4 * pictures(d["x"]) * m.reshape(-1)).astype(np.float32)); return d
def setup_inputs_clear(rng):
    d = setup_inputs(rng); o = rng.permutation(16); mu = d["mu"].copy(); mu[:, o[:5]] = 0
    mu[:, o[5:9]] = np.minimum(rng.random((N, 4, H * D)) + 0.5, 1).astype(np.float32); d["mu"] = mu
    c = d["counts"].reshape(N, 8, 16, B * D).copy(); c[:, :, o[3:7]] = 0; d["counts"] = c.reshape(N, 128, B * D); return d
def setup_inputs_spread(rng):
    d = setup_inputs(rng); d["x"] = wide(rng, N, 16, H * D).astype(np.float32)
    d["counts"] = wide(rng, N, 128, B * D).astype(np.float32) * np.float32(64); return d
def check_inputs(d):
    bad = [k for k in ("x", "counts") if not np.isfinite(d[k]).all()]
    m = d["mu"]; a = d["ang"]; g = a.reshape(N, 8, 16, 2 * B)
    if not (np.isfinite(m).all() and (m >= 0).all() and (m <= 1).all()): bad.append("mu between 0 and 1")
    if ((a < -256) | (a > 256)).any(): bad.append("ang between -256 and 256")
    if (g != g[:, :, :1]).any(): bad.append("ang alike in a group")
    return bad
def cells(c, sn):
    a = 2 * np.arange(D)[None, None, :] - (D - 1); b = 2 * np.arange(D)[None, :, None] - (D - 1)
    c = c[:, None, None]; sn = sn[:, None, None]
    col = (c * a - sn * b + 256 * D) >> 9; row = (sn * a + c * b + 256 * D) >> 9
    ok = (col >= 0) & (col < D) & (row >= 0) & (row < D)
    return np.where(ok, D * row + col, D * D).reshape(-1, D * D)
def zero_end(v):
    return np.concatenate([v, np.zeros((16, 1))], 1)
def reference(x, mu, counts, ang):
    cs = ang.reshape(N, 8, 16, B, 2)[:, :, 0].transpose(0, 2, 1, 3).reshape(-1, 2).astype(np.int64)
    cnt = counts.reshape(N, 8, 16, B, D).transpose(0, 3, 1, 2, 4).reshape(-1, 16, D).astype(np.float64)
    there = cells(cs[:, 0], cs[:, 1]); back = cells(cs[:, 0], -cs[:, 1]); A = len(cs)
    M = zero_end(pictures(mu).astype(np.float64)); X = pictures(x).astype(np.float64)
    W = [np.exp(-np.add.accumulate(np.take(M, there[a], axis=1).reshape(16, D, D), axis=1)) for a in range(A)]
    for k in range(R):
        Z = zero_end(X); G = np.zeros((16, D * D))
        for a in range(A):
            e = cnt[a] - np.add.reduce(W[a] * np.take(Z, there[a], axis=1).reshape(16, D, D), axis=1)
            G += np.take(zero_end((W[a] * e[:, None, :]).reshape(16, D * D)), back[a], axis=1)
        X = np.maximum(X + STEP * G, 0)
    return {"y": stripes(X).astype(np.float32)}

@@ -1,0 +1,396 @@
+from concourse.bass import DstId, RemoteDMATransfer
+from concourse.mybir import AluOpType as A, ActivationFunctionType as AF
+
+R = 3
+STEP = 2.0 ** -12
+STAGES = [(0, 0, 512), (1, 0, 512)]
+LAG = 1536
+WBV = 5
+PLP = 3
+DCH = [("v", 52, 64), ("s", 0, 14), ("s", 14, 28), ("s", 28, 42), ("s", 42, 52)]
+TAIL = [("c", 0), ("c", 1), ("n", 0), ("n", 1)]
+KQ = 0.00012918686694904754
+QUAD = [(1.1219518404595346, 18.754011438386996), (-4.267052247540635, 2.746736091488364),
+        (-1.8906565018022652, 14.883958171039492)]
+SCRATCH = {}
+for _n, _w in (("mc", 64), ("dx", 128), ("pdx", 128), ("angf", 4), ("cnt", 64), ("sq", 192), ("rq", 320),
+               ("rep", 1024), ("ssum", 16), ("ssel", 16), ("fm", 1), ("a64", 64), ("b4i", 4), ("b4", 4), ("kc", 4),
+               ("kr", 4), ("pen", 256), ("raw", 256), ("raw2", 256), ("D", 4104), ("X", 4104), ("W", 4104), ("f", 4104),
+               ("ind", 1024), ("xg", 4096), ("st", 4096), ("wb", 4096), ("pr", 4096), ("eg", 3072), ("u", 64), ("e", 64),
+               ("snd", 1536), ("lnd", 1152), ("t1", 64), ("t2", 64), ("pt", 384), ("xs", 384), ("rp", 1024), ("ysb", 512),
+               ("d0", 64), ("old", 128)):
+    SCRATCH[_n] = ("sbuf", [128, _w], "float32")
+for _n, _w in (("angi", 2), ("ipz", 16), ("ipz2", 16), ("ip", 1), ("ip2", 1), ("vc", 256), ("vr", 256), ("col", 256),
+               ("row", 256), ("tp", 256)):
+    SCRATCH[_n] = ("sbuf", [128, _w], "int32")
+for _n in ("fl", "tl"):
+    SCRATCH[_n] = ("sbuf", [128, 256], "uint16")
+for _n in range(8):
+    SCRATCH["bank%d" % _n] = ("psum", [128, 512], "float32")
+SEMAPHORES = (["v", "s", "p", "q", "ldm", "ldx", "lda", "ldc", "yo", "cx", "cd", "lr"]
+              + ["pd0", "pd1", "pw0", "pw1", "ld0", "ld1", "lw0", "lw1"]
+              + ["%s_%d_%d" % (n, k, s) for n in ("rs", "xc", "pu", "lp") for k in range(R) for s in range(len(STAGES))])
+
+
+def ts(out, i, s1, o0, s2=None, o1=None):
+    if o1 is None:
+        return lambda e: e.tensor_scalar(out, i, s1, None, o0)
+    return lambda e: e.tensor_scalar(out, i, s1, s2, o0, o1)
+
+
+def tt(out, a, b, o):
+    return lambda e: e.tensor_tensor(out, a, b, o)
+
+
+def cp(out, i):
+    return lambda e: e.tensor_copy(out, i)
+
+
+def act(out, i, fn=AF.Copy, scale=1.0):
+    return lambda e: e.activation(out, i, fn, scale=scale)
+
+
+def mm(out, l, r, a, z):
+    return lambda e: e.matmul(out, l, r, a, z)
+
+
+def ms(ap, c):
+    return lambda e: e.memset(ap, c)
+
+
+def scan(out, d0, d1, o0=A.mult, o1=A.add):
+    return lambda e: e.tensor_tensor_scan(out, d0, d1, 0.0, o0, o1)
+
+
+def rank_program(g, core, T, topo):
+    rank = T.rank_of(core)
+    if rank is None:
+        return
+    chips = []
+    for c in T.cores:
+        if topo.chip(c) not in chips:
+            chips.append(topo.chip(c))
+    members = [[r for r, c in enumerate(T.cores) if topo.chip(c) == ch] for ch in chips]
+    ci = chips.index(topo.chip(core))
+    mine = members[ci]
+    me = mine.index(rank)
+    NQ = len(mine)
+    NS = len(STAGES)
+    partner = members[1 - ci][me]
+    peers = [mine[(me + k) % NQ] for k in range(1, NQ)]
+    on_mask = topo.mask(core, T.cores[peers[0]])
+    ne_on = len(topo.engines(core, T.cores[peers[0]]))
+    ne_off = len(topo.engines(core, T.cores[partner]))
+    npush = ne_on * (NQ - 1)
+
+    ENG = {"v": g.vector, "s": g.scalar, "p": g.tensor, "q": g, "y": g.sync}
+    cnt, known, touch, sent, hist = {}, {}, {}, {}, {}
+
+    def wait(eng, sem, val):
+        if known.get((eng, sem), 0) < val:
+            ENG[eng].wait_ge(T.sem[sem], val)
+            known[(eng, sem)] = val
+
+    def waits(eng, deps):
+        for d in deps:
+            if d is not None:
+                wait(eng, d[0], d[1])
+
+    def op(eng, fn, deps=(), bank=None):
+        waits(eng, deps)
+        use = touch.setdefault(bank, {}) if bank is not None else {}
+        for (o, n) in use.items():
+            if o != eng:
+                wait(eng, o, n)
+        fn(ENG[eng]).then_inc(T.sem[eng], 1)
+        cnt[eng] = cnt.get(eng, 0) + 1
+        use[eng] = cnt[eng]
+        return (eng, cnt[eng])
+
+    def load(eng, out, in_, sem):
+        ENG[eng].dma_start(out, in_).then_inc(T.sem[sem], 16)
+        hist[sem] = hist.get(sem, 0) + 16
+        return (sem, hist[sem])
+
+    def send(dst, out, in_, rsem, deps):
+        waits("q", deps)
+        c = T.cores[dst]
+        rid, pid, _ = topo.addr(c)
+        g.remote_dma(out, in_, T.sem[rsem], T.sem.lr, pid, rid, topo.mask(core, c))
+        sent["lr"] = sent.get("lr", 0) + len(topo.engines(core, c))
+
+    def push(ap, rsem, lsem, deps):
+        waits("q", deps)
+        ids = [DstId(rid=topo.addr(T.cores[r])[0], pnc=topo.addr(T.cores[r])[1]) for r in peers]
+        g.remote_dma_fused([RemoteDMATransfer(dst_ids=ids, dma_engine_mask=on_mask, remote_sem=T.sem[rsem], srcs=[ap],
+                                              dsts=[ap] * len(peers), alu_op=0)], local_sem=T.sem[lsem])
+        sent[lsem] = sent.get(lsem, 0) + ne_on
+
+    PB = [T["bank%d" % i] for i in range(8)]
+    eye = T.rep[:, 0:128]
+
+    dm = load("y", T.mc[:], T.mu[:], "ldm")
+    dxl = load("s", T.dx[:, 64:128], T.x[:], "ldx")
+    da = load("y", T.angi[:], T.ang[:], "lda")
+    dc = load("y", T.cnt[:], T.counts[:], "ldc")
+    ones = op("v", ms(eye, 1.0))
+    c_eye = op("q", lambda e: e.affine_select(eye, eye, [[-1, 128]], A.is_equal, 0.0, 0, 1), [ones])
+    c_p = op("q", lambda e: e.iota(T.ip[:], [[0, 1]], 0, 1))
+    c_a = op("q", lambda e: e.iota(T.a64[:], [[2, 64]], -63, 0, allow_small_or_imprecise_dtypes=True))
+    c_b = op("q", lambda e: e.iota(T.b4i[:], [[32, 4]], 0, 0, allow_small_or_imprecise_dtypes=True))
+    c_z = op("q", lambda e: e.iota(T.ipz[:], [[-1, 16]], 0, 1))
+    tails = [op("v", ms(T.D[:, 4096:4104], 1.0))]
+    for b in (T.X, T.W, T.f):
+        tails.append(op("v", ms(b[:, 4096:4104], 0.0)))
+    c_rep = [c_eye]
+    for j in range(1, 8):
+        o = T.rep[:, 128 * j:128 * j + 128]
+        c_rep.append(op("v", cp(o, eye), [c_eye]) if j < 5 else op("s", act(o, eye), [c_eye]))
+    send(partner, T.pdx[:, 64:128], T.dx[:, 64:128], "cx", [dxl])
+
+    sq = [T.sq[:, 64 * i:64 * i + 64] for i in range(3)]
+    rq = [T.rq[:, 64 * i:64 * i + 64] for i in range(5)]
+    sb = [op("v", ts(sq[i], T.mc[:], QUAD[i][0], A.add), [dm]) for i in range(3)]
+    ss = [op("s", act(sq[i], sq[i], AF.Square), [sb[i]]) for i in range(3)]
+    r0 = op("v", ts(rq[0], sq[0], QUAD[0][1], A.add, -KQ, A.mult), [ss[0]])
+    r1 = op("v", ts(rq[1], sq[1], QUAD[1][1], A.add), [ss[1]])
+    r2 = op("v", ts(rq[2], sq[2], QUAD[2][1], A.add), [ss[2]])
+    r0 = op("v", tt(rq[3], rq[0], T.mc[:], A.mult), [r0])
+    r3 = op("v", tt(rq[4], rq[1], rq[2], A.mult), [r1, r2])
+    r4 = op("v", tt(sq[0], rq[4], rq[3], A.mult), [r0, r3])
+    d_c = op("v", ts(T.dx[:, 0:64], sq[0], 1.0, A.add), [r4])
+    send(partner, T.pdx[:, 0:64], T.dx[:, 0:64], "cd", [d_c])
+
+    def blk(win, q, h0=0, h1=512):
+        return win[:, 512 * q + h0:512 * q + h1]
+
+    def spread(src, k, deps=()):
+        return [[op("p", mm(PB[2 * k + half][:, 64 * h:64 * h + 64], T.rep[:, 4 * half + h:1024:8], src, True, True),
+                    c_rep + list(deps), 2 * k + half) for h in range(4)][-1] for half in range(2)]
+
+    def settle(win, q, k, m):
+        return [op("v", cp(blk(win, q, 0, 256), PB[2 * k][:, 0:256]), [m[0]], 2 * k),
+                op("s", act(blk(win, q, 256, 512), PB[2 * k + 1][:, 0:256]), [m[1]], 2 * k + 1)]
+
+    m_d = spread(T.dx[:, 0:64], 0, [d_c])
+    m_x = spread(T.dx[:, 64:128], 1, [dxl])
+
+    a0 = op("v", cp(T.angf[:, 0:2], T.angi[:]), [da])
+    a1 = op("v", ts(T.ip2[:], T.ip[:], 15, A.bitwise_and), [c_p])
+    a2 = op("v", ts(T.angf[:, 2:3], T.angf[:, 1:2], -1.0, A.mult), [a0])
+    a3 = op("v", ts(T.fm[:], T.ip2[:], 2.0, A.mult, -63.0, A.add), [a1])
+    a4 = op("v", ts(T.b4[:], T.b4i[:], T.fm[:, 0:1], A.add), [a3, c_b])
+    a5 = op("v", ts(T.kc[:], T.b4[:], T.angf[:, 2:3], A.mult, 16384.0, A.add), [a4, a2])
+    a6 = op("v", ts(T.kr[:], T.b4[:], T.angf[:, 0:1], A.mult, 16384.0, A.add), [a4])
+    e_d = settle(T.D, rank, 0, m_d)
+    push(blk(T.D, rank), "pd0", "ld0", e_d)
+    for k in range(4):
+        lc = op("v", ts(T.vc[:, k:256:4], T.a64[:], T.angf[:, 0:1], A.mult, T.kc[:, k:k + 1], A.add), [a5, c_a])
+        lr = op("v", ts(T.vr[:, k:256:4], T.a64[:], T.angf[:, 1:2], A.mult, T.kr[:, k:k + 1], A.add), [a6, c_a])
+    c1 = op("v", ts(T.col[:], T.vc[:], 9, A.logical_shift_right), [lc])
+    c2 = op("v", ts(T.row[:], T.vr[:], 3, A.logical_shift_right, 0x1FFFFFC0, A.bitwise_and), [lr])
+    c3 = op("v", ts(T.pen[:], T.col[:], 64.0, A.is_ge, 4096.0, A.mult), [c1])
+    c4 = op("v", tt(T.raw[:], T.col[:], T.row[:], A.add), [c1, c2])
+    wait("p", "cd", ne_off)
+    m_dp = spread(T.pdx[:, 0:64], 2)
+    wait("p", "cx", ne_off)
+    m_xp = spread(T.pdx[:, 64:128], 3)
+    e_dp = settle(T.D, partner, 2, m_dp)
+    push(blk(T.D, partner), "pd1", "ld1", e_dp)
+    e_d += e_dp
+    e_x = settle(T.X, rank, 1, m_x)
+    push(blk(T.X, rank), "pw0", "lw0", e_x)
+    e_xp = settle(T.X, partner, 3, m_xp)
+    push(blk(T.X, partner), "pw1", "lw1", e_xp)
+    ev = e_x + e_xp
+    c6 = op("v", tt(T.raw2[:], T.raw[:], T.pen[:], A.add), [c3, c4])
+    fl = op("v", ts(T.fl[:], T.raw2[:], 4096.0, A.min), [c6])
+    in0 = op("v", ms(T.ind[:], 0.0))
+    in1 = op("v", ms(T.ind[:, 0:1024:64], 1.0), [in0])
+    c5 = op("v", ts(T.tp[:], T.vr[:], 9, A.arith_shift_right), [lr])
+    tl = op("v", ts(T.tl[:], T.tp[:], 0.0, A.max, 63.0, A.min), [c5])
+    s_1 = op("v", ts(T.ipz2[:], T.ipz[:], 15, A.bitwise_and), [c_z])
+    s_sel = op("v", ts(T.ssel[:], T.ipz[:], 0.0, A.is_equal, 2048.0, A.mult), [c_z])
+    s_sum = op("v", ts(T.ssum[:], T.ipz2[:], 0.0, A.is_equal), [s_1])
+
+    Ew = T.e[:, 0:64]
+
+    def gath(eng, out, win, off, deps):
+        src = win.indirect(off)
+        return op(eng, cp(out, src) if eng == "v" else act(out, src), deps)
+
+    for eng in ("s", "v"):
+        wait(eng, "pd0", npush)
+        wait(eng, "pd1", npush)
+
+    dg = {a: gath(eng, T.f[:, 64 * a:64 * z], T.D[:], T.fl[:, 4 * a:4 * z], [fl] + e_d + tails) for eng, a, z in DCH}
+    wsc = []
+    for eng, a, z in DCH:
+        wsc.append(op("v", scan(T.W[:, 64 * a:64 * z], T.ind[:, 0:64 * (z - a)], T.f[:, 64 * a:64 * z], A.max, A.mult),
+                      [dg[a], in1]))
+    d0 = op("v", cp(T.d0[:], T.f[:, 0:4096:64]), wsc)
+    fz = op("v", ms(T.f[:, 0:4096:64], 0.0), [d0])
+
+    def order(k):
+        idx = list(range(NS))
+        if k == R - 1:
+            idx.sort(key=lambda i: STAGES[i][0] == ci)
+        return idx
+
+    def chunk(i, n):
+        s, lo, hi = STAGES[i]
+        return 512 * members[s][(me + 1 + n) % NQ] + lo, hi - lo
+
+    at, room = {}, 0
+    for i in order(0):
+        for n in range(1, NQ):
+            at[(i, n)] = room
+            room += chunk(i, n)[1]
+    soff = [sum(h - l for _, l, h in STAGES[:i]) // 8 for i in range(NS)]
+
+    def xgath(eng, a, z):
+        return (a, z, gath(eng, T.xg[:, 64 * a:64 * z], T.X[:], T.fl[:, 4 * a:4 * z], [fl] + ev + tails))
+
+    def hscan(a, z, dep):
+        lo = 64 * a - 1 if a else None
+        return op("v", scan(T.st[:, 64 * z - 1:lo:-1], T.f[:, 64 * z:64 * a:-1], T.xg[:, 64 * z - 1:lo:-1]), [dep, fz])
+
+    wbg, loc, run = {}, {}, [0]
+    for k in range(R):
+        last = k == R - 1
+        for eng in ("s", "v"):
+            for n in ["pu_%d_%d" % (k - 1, i) for i in range(NS)] if k else ["pw0", "pw1"]:
+                wait(eng, n, npush)
+        ordr = order(k)
+        seq = [(i, n) for i in ordr for n in range(NQ)]
+        for i in ordr:
+            p, w = chunk(i, NQ - 1)
+            nb = w // 128
+            for b in range(nb):
+                mo = op("p", mm(PB[0][:, soff[i] + b:soff[i] + 16 * nb:nb], T.X[:, p + 128 * b:p + 128 * b + 128],
+                                T.ssel[:], True, True), [s_sel] + ev, 0)
+        if k == 0:
+            sc = [xgath("s", a, a + 16) for a in range(0, 64, 16)]
+            done = 0
+            for c in seq:
+                p, w = chunk(*c)
+                wbg[c] = gath("v" if done < 512 * WBV else "s", T.wb[:, p:p + w], T.W[:], T.fl[:, p // 16:(p + w) // 16],
+                              wsc + tails)
+                done += w
+            hs = [hscan(*c) for c in sc]
+        else:
+            sc = [xgath("s", a, z) for a, z in ((14, 26), (26, 38), (38, 50), (50, 60), (60, 64))]
+            va = xgath("v", 0, 8)
+            hs = [hscan(*va), hscan(*sc[0])]
+            vb = xgath("v", 8, 14)
+            hs += [hscan(*c) for c in [sc[1], vb] + sc[2:]]
+        om = op("s", act(T.old[:], PB[0][:, 0:128]), [mo, hist.get("old")], 0)
+        e0 = op("v", tt(T.u[:], T.d0[:], T.st[:, 0:4096:64], A.mult), hs + [d0])
+        ee = op("v", tt(T.e[:], T.cnt[:], T.u[:], A.subtract), [e0, dc])
+
+        def place(c, eng):
+            p, w = chunk(*c)
+            b, o = 2 + at[c] // 512, at[c] % 512
+            o = PB[b][:, o:o + w]
+            loc[c] = op(eng, mm(o, eye, T.wb[:, p:p + w], True, True) if eng == "p" else act(o, T.wb[:, p:p + w]), [wbg[c]], b)
+
+        egd, bsum, part, pts = {}, {}, {}, {}
+        inp = [c for c in seq if c in at]
+        if k == 0:
+            for c in inp[:PLP]:
+                place(c, "p")
+        for c in inp:
+            if c not in loc:
+                place(c, "s")
+            p, w = chunk(*c)
+            egd[c] = gath("s", T.eg[:, at[c]:at[c] + w], Ew, T.tl[:, p // 16:(p + w) // 16], [ee, tl])
+
+        def evac(n):
+            c = seq[n]
+            i, w = c[0], chunk(*c)[1] // 8
+            o = T.snd[:, run[0]:run[0] + w]
+            run[0] += w
+            if c[1] == NQ - 1:
+                d = hist["old"] = op("v", tt(o, PB[n % 2][:, 0:w], T.old[:, soff[i]:soff[i] + w], A.add), [bsum[c], om], n % 2)
+            else:
+                d = op("v", cp(o, PB[n % 2][:, 0:w]), [bsum[c]], n % 2)
+                m = 3 * (128 * k + soff[i]) + c[1] * w
+                send(peers[c[1]], T.lnd[:, m:m + w], o, "rs_%d_%d" % (k, i), [d])
+            part[c] = (o, d)
+
+        def chipsum(i):
+            w = chunk(i, 0)[1] // 8
+            m = 128 * k + soff[i]
+            wait("v", "rs_%d_%d" % (k, i), npush)
+            a = op("v", tt(T.t1[:, 0:w], T.lnd[:, 3 * m:3 * m + w], T.lnd[:, 3 * m + w:3 * m + 2 * w], A.add), [hist.get("pt")])
+            o, d = part[(i, NQ - 1)]
+            b = op("v", tt(T.t2[:, 0:w], T.lnd[:, 3 * m + 2 * w:3 * m + 3 * w], o, A.add), [d])
+            hist["pt"] = pts[i] = op("v", tt(T.pt[:, m:m + w], T.t1[:, 0:w], T.t2[:, 0:w], A.add), [a, b])
+            if not last or STAGES[i][0] != ci:
+                send(partner, T.xs[:, m:m + w], T.pt[:, m:m + w], "xc_%d_%d" % (k, i), [pts[i]])
+
+        evs = []
+
+        def newact(i):
+            p, w = chunk(i, NQ - 1)
+            nb, w8, m, r, h = w // 128, w // 8, 128 * k + soff[i], 8 * soff[i], w // 2
+            wait("v", "xc_%d_%d" % (k, i), ne_off)
+            n = op("v", tt(T.rp[:, r:r + w8], T.pt[:, m:m + w8], T.xs[:, m:m + w8], A.add), [pts[i], hist.get(i)])
+            cps, rows, win, lo = [n], 16, T.ysb, p % 512
+            if not last:
+                rows, win, lo = 128, T.X, p
+                for j in range(1, 8):
+                    o, f = T.rp[:, r + w8 * j:r + w8 * j + w8], T.rp[:, r:r + w8]
+                    cps.append(op("v", cp(o, f), [n]) if j < 4 else op("s", act(o, f), [n]))
+                for eng in ("v", "s"):
+                    for b in ["lp_%d_%d" % (k - 1, i)] if k else ["lw0", "lw1"]:
+                        wait(eng, b, ne_on)
+            hb = nb // 2
+            tp = [op("p", mm(PB[b // hb][0:rows, 128 * (b % hb):128 * (b % hb) + 128], T.rp[:, r + b:r + rows * nb:nb], eye,
+                             True, True), cps + [c_eye], b // hb) for b in range(nb)]
+            hist[i] = tp[-1]
+            ab = [op("v", ts(win[0:rows, lo:lo + h], PB[0][0:rows, 0:h], STEP, A.mult, 0.0, A.max), [tp[hb - 1]], 0),
+                  op("s", act(win[0:rows, lo + h:lo + w], PB[1][0:rows, 0:h], AF.Relu, STEP), [tp[-1]], 1)]
+            if last:
+                waits("y", ab)
+                load("y", T.y[:, lo:lo + w], T.ysb[0:16, lo:lo + w], "yo")
+            else:
+                push(T.X[:, p:p + w], "pu_%d_%d" % (k, i), "lp_%d_%d" % (k, i), ab)
+                evs.extend(ab)
+
+        due, todo = {}, list(ordr)
+        for n, c in enumerate(seq):
+            p, w = chunk(*c)
+            out = T.pr[:, p:p + w]
+            if c in at:
+                b, r = 2 + at[c] // 512, at[c] % 512
+                pd = op("v", tt(out, T.eg[:, at[c]:at[c] + w], PB[b][:, r:r + w], A.mult), [egd[c], loc[c]], b)
+            else:
+                pd = op("v", tt(out, Ew.indirect(T.tl[:, p // 16:(p + w) // 16]), T.wb[:, p:p + w], A.mult), [ee, wbg[c], tl])
+            nb = w // 128
+            for b in range(nb):
+                bsum[c] = op("p", mm(PB[n % 2][:, b:16 * nb:nb], T.pr[:, p + 128 * b:p + 128 * b + 128], T.ssum[:], True, True),
+                             [pd, s_sum], n % 2)
+            if n:
+                evac(n - 1)
+            for i in due:
+                due[i] += w
+            if c[1] == NQ - 1:
+                due[c[0]] = 0
+            while todo and due.get(todo[0], -1) >= LAG:
+                chipsum(todo.pop(0))
+        evac(len(seq) - 1)
+        for what, j in TAIL:
+            i = ordr[j]
+            if what == "c" and i in todo:
+                chipsum(i)
+            if what == "n" and (not last or STAGES[i][0] == ci):
+                newact(i)
+        ev = evs
+
+    for e in ("v", "s", "p", "q"):
+        wait("q", e, cnt[e])
+    for n in sorted(sent):
+        wait("q", n, sent[n])
+    for n in ("ldm", "ldx", "lda", "ldc", "yo"):
+        wait("q", n, hist[n])

@@ -3,12 +3,11 @@ from concourse.mybir import AluOpType as A, ActivationFunctionType as AF
 
 R = 3
 STEP = 2.0 ** -12
-STAGES = [(0, 0, 512), (1, 0, 512)]
-LAG = 1536
+STAGES = [(1, 0, 256), (1, 256, 512), (0, 0, 512)]
+FUSED = [(0, 1), (1, 1), (1, 0)]
+WORDER = [(2, 1), (3, 1), (2, 0), (3, 0), (1, 1), (1, 0), (0, 0), (0, 1)]
 WBV = 5
-PLP = 3
 DCH = [("v", 52, 64), ("s", 0, 14), ("s", 14, 28), ("s", 28, 42), ("s", 42, 52)]
-TAIL = [("c", 0), ("c", 1), ("n", 0), ("n", 1)]
 KQ = 0.00012918686694904754
 QUAD = [(1.1219518404595346, 18.754011438386996), (-4.267052247540635, 2.746736091488364),
         (-1.8906565018022652, 14.883958171039492)]
@@ -16,20 +15,22 @@ SCRATCH = {}
 for _n, _w in (("mc", 64), ("dx", 128), ("pdx", 128), ("angf", 4), ("cnt", 64), ("sq", 192), ("rq", 320),
                ("rep", 1024), ("ssum", 16), ("ssel", 16), ("fm", 1), ("a64", 64), ("b4i", 4), ("b4", 4), ("kc", 4),
                ("kr", 4), ("pen", 256), ("raw", 256), ("raw2", 256), ("D", 4104), ("X", 4104), ("W", 4104), ("f", 4104),
-               ("ind", 1024), ("xg", 4096), ("st", 4096), ("wb", 4096), ("pr", 4096), ("eg", 3072), ("u", 64), ("e", 64),
-               ("snd", 1536), ("lnd", 1152), ("t1", 64), ("t2", 64), ("pt", 384), ("xs", 384), ("rp", 1024), ("ysb", 512),
-               ("d0", 64), ("old", 128)):
+               ("ind", 1024), ("xg", 4096), ("st", 4096), ("wb", 4096), ("wl", 3072), ("pr", 4096), ("eg", 4096), ("u", 64),
+               ("el", 768), ("pt", 384), ("xs", 384), ("rp", 1024), ("ptr", 1024), ("ysb", 512), ("d0", 64), ("zer", 64),
+               ("p16", 1), ("rli", 48)):
     SCRATCH[_n] = ("sbuf", [128, _w], "float32")
 for _n, _w in (("angi", 2), ("ipz", 16), ("ipz2", 16), ("ip", 1), ("ip2", 1), ("vc", 256), ("vr", 256), ("col", 256),
                ("row", 256), ("tp", 256)):
     SCRATCH[_n] = ("sbuf", [128, _w], "int32")
-for _n in ("fl", "tl"):
-    SCRATCH[_n] = ("sbuf", [128, 256], "uint16")
+for _n, _w in (("fl", 256), ("tl", 256), ("tll", 192), ("rl", 48)):
+    SCRATCH[_n] = ("sbuf", [128, _w], "uint16")
 for _n in range(8):
     SCRATCH["bank%d" % _n] = ("psum", [128, 512], "float32")
-SEMAPHORES = (["v", "s", "p", "q", "ldm", "ldx", "lda", "ldc", "yo", "cx", "cd", "lr"]
+SEMAPHORES = (["v", "s", "p", "q", "ldm", "ldx", "lda", "ldc", "yo", "cx", "cd", "lr", "tx"]
               + ["pd0", "pd1", "pw0", "pw1", "ld0", "ld1", "lw0", "lw1"]
-              + ["%s_%d_%d" % (n, k, s) for n in ("rs", "xc", "pu", "lp") for k in range(R) for s in range(len(STAGES))])
+              + ["wx_%d_%d" % (j, s) for j in range(1, 4) for s in range(2)]
+              + ["ex_%d" % k for k in range(R)]
+              + ["%s_%d_%d" % (n, k, s) for n in ("xc", "pu", "lp") for k in range(R) for s in range(len(STAGES))])
 
 
 def ts(out, i, s1, o0, s2=None, o1=None):
@@ -75,11 +76,11 @@ def rank_program(g, core, T, topo):
     mine = members[ci]
     me = mine.index(rank)
     NQ = len(mine)
-    NS = len(STAGES)
     partner = members[1 - ci][me]
     peers = [mine[(me + k) % NQ] for k in range(1, NQ)]
     on_mask = topo.mask(core, T.cores[peers[0]])
-    ne_on = len(topo.engines(core, T.cores[peers[0]]))
+    on_eng = topo.engines(core, T.cores[peers[0]])
+    ne_on = len(on_eng)
     ne_off = len(topo.engines(core, T.cores[partner]))
     npush = ne_on * (NQ - 1)
 
@@ -119,11 +120,12 @@ def rank_program(g, core, T, topo):
         g.remote_dma(out, in_, T.sem[rsem], T.sem.lr, pid, rid, topo.mask(core, c))
         sent["lr"] = sent.get("lr", 0) + len(topo.engines(core, c))
 
-    def push(ap, rsem, lsem, deps):
+    ids = [DstId(rid=topo.addr(T.cores[r])[0], pnc=topo.addr(T.cores[r])[1]) for r in peers]
+
+    def push(ap, rsem, lsem, deps, dsts=None):
         waits("q", deps)
-        ids = [DstId(rid=topo.addr(T.cores[r])[0], pnc=topo.addr(T.cores[r])[1]) for r in peers]
         g.remote_dma_fused([RemoteDMATransfer(dst_ids=ids, dma_engine_mask=on_mask, remote_sem=T.sem[rsem], srcs=[ap],
-                                              dsts=[ap] * len(peers), alu_op=0)], local_sem=T.sem[lsem])
+                                              dsts=dsts or [ap] * len(peers), alu_op=0)], local_sem=T.sem[lsem])
         sent[lsem] = sent.get(lsem, 0) + ne_on
 
     PB = [T["bank%d" % i] for i in range(8)]
@@ -138,10 +140,10 @@ def rank_program(g, core, T, topo):
     c_p = op("q", lambda e: e.iota(T.ip[:], [[0, 1]], 0, 1))
     c_a = op("q", lambda e: e.iota(T.a64[:], [[2, 64]], -63, 0, allow_small_or_imprecise_dtypes=True))
     c_b = op("q", lambda e: e.iota(T.b4i[:], [[32, 4]], 0, 0, allow_small_or_imprecise_dtypes=True))
-    c_z = op("q", lambda e: e.iota(T.ipz[:], [[-1, 16]], 0, 1))
     tails = [op("v", ms(T.D[:, 4096:4104], 1.0))]
     for b in (T.X, T.W, T.f):
         tails.append(op("v", ms(b[:, 4096:4104], 0.0)))
+    c_0 = op("v", ms(T.zer[:], 0.0))
     c_rep = [c_eye]
     for j in range(1, 8):
         o = T.rep[:, 128 * j:128 * j + 128]
@@ -160,6 +162,7 @@ def rank_program(g, core, T, topo):
     r4 = op("v", tt(sq[0], rq[4], rq[3], A.mult), [r0, r3])
     d_c = op("v", ts(T.dx[:, 0:64], sq[0], 1.0, A.add), [r4])
     send(partner, T.pdx[:, 0:64], T.dx[:, 0:64], "cd", [d_c])
+    c_z = op("q", lambda e: e.iota(T.ipz[:], [[-1, 16]], 0, 1))
 
     def blk(win, q, h0=0, h1=512):
         return win[:, 512 * q + h0:512 * q + h1]
@@ -184,6 +187,8 @@ def rank_program(g, core, T, topo):
     a6 = op("v", ts(T.kr[:], T.b4[:], T.angf[:, 0:1], A.mult, 16384.0, A.add), [a4])
     e_d = settle(T.D, rank, 0, m_d)
     push(blk(T.D, rank), "pd0", "ld0", e_d)
+    c_r = [op("q", lambda e: e.iota(T.rli[:, 0:16], [[0, 8], [16, 2]], 0, 0, allow_small_or_imprecise_dtypes=True)),
+           op("q", lambda e: e.iota(T.rli[:, 16:48], [[0, 8], [16, 4]], 0, 0, allow_small_or_imprecise_dtypes=True))]
     for k in range(4):
         lc = op("v", ts(T.vc[:, k:256:4], T.a64[:], T.angf[:, 0:1], A.mult, T.kc[:, k:k + 1], A.add), [a5, c_a])
         lr = op("v", ts(T.vr[:, k:256:4], T.a64[:], T.angf[:, 1:2], A.mult, T.kr[:, k:k + 1], A.add), [a6, c_a])
@@ -212,8 +217,28 @@ def rank_program(g, core, T, topo):
     s_1 = op("v", ts(T.ipz2[:], T.ipz[:], 15, A.bitwise_and), [c_z])
     s_sel = op("v", ts(T.ssel[:], T.ipz[:], 0.0, A.is_equal, 2048.0, A.mult), [c_z])
     s_sum = op("v", ts(T.ssum[:], T.ipz2[:], 0.0, A.is_equal), [s_1])
+    p16 = op("v", cp(T.p16[:], T.ip2[:]), [a1])
+    rl = op("v", ts(T.rl[:], T.rli[:], T.p16[:, 0:1], A.add), c_r + [p16])
+    RL = {32: T.rl[:, 0:16], 64: T.rl[:, 16:48]}
 
-    Ew = T.e[:, 0:64]
+    def theirs(j, s):
+        return members[s][(me + j) % NQ]
+
+    def wsrc(j, s, lo, hi):
+        return blk(T.wb, theirs(0, s), lo, hi) if j == 0 else blk(T.wl, 2 * (j - 1) + s, lo, hi)
+
+    def rays(j, s, lo, hi):
+        t, b = (T.tl, theirs(0, s)) if j == 0 else (T.tll, 2 * (j - 1) + s)
+        return t[:, 32 * b + lo // 16:32 * b + hi // 16]
+
+    waits("q", [tl])
+    pairs = [(j, s) for j in range(1, NQ) for s in range(2)]
+    per = ne_on // 8
+    g.remote_dma_fused([RemoteDMATransfer(
+        dst_ids=[ids[j - 1]], dma_engine_mask=sum(1 << e for e in on_eng[per * n:per * n + per]), remote_sem=T.sem.tx,
+        srcs=[T.tl[:, 32 * theirs(j, s):32 * theirs(j, s) + 32]], dsts=[rays(j, s, 0, 512)], alu_op=0)
+        for n, (j, s) in enumerate(pairs)], local_sem=T.sem.lr)
+    sent["lr"] += per * len(pairs)
 
     def gath(eng, out, win, off, deps):
         src = win.indirect(off)
@@ -231,23 +256,6 @@ def rank_program(g, core, T, topo):
     d0 = op("v", cp(T.d0[:], T.f[:, 0:4096:64]), wsc)
     fz = op("v", ms(T.f[:, 0:4096:64], 0.0), [d0])
 
-    def order(k):
-        idx = list(range(NS))
-        if k == R - 1:
-            idx.sort(key=lambda i: STAGES[i][0] == ci)
-        return idx
-
-    def chunk(i, n):
-        s, lo, hi = STAGES[i]
-        return 512 * members[s][(me + 1 + n) % NQ] + lo, hi - lo
-
-    at, room = {}, 0
-    for i in order(0):
-        for n in range(1, NQ):
-            at[(i, n)] = room
-            room += chunk(i, n)[1]
-    soff = [sum(h - l for _, l, h in STAGES[:i]) // 8 for i in range(NS)]
-
     def xgath(eng, a, z):
         return (a, z, gath(eng, T.xg[:, 64 * a:64 * z], T.X[:], T.fl[:, 4 * a:4 * z], [fl] + ev + tails))
 
@@ -255,138 +263,139 @@ def rank_program(g, core, T, topo):
         lo = 64 * a - 1 if a else None
         return op("v", scan(T.st[:, 64 * z - 1:lo:-1], T.f[:, 64 * z:64 * a:-1], T.xg[:, 64 * z - 1:lo:-1]), [dep, fz])
 
-    wbg, loc, run = {}, {}, [0]
+    placed = [c for c in WORDER if c not in FUSED]
+    have, loc = {}, {}
+
+    def wgath(eng, j, s):
+        b = theirs(j, s)
+        d = gath(eng, blk(T.wb, b), T.W[:], T.fl[:, 32 * b:32 * b + 32], wsc + tails)
+        if j:
+            send(peers[j - 1], wsrc(j, s, 0, 512), blk(T.wb, b), "wx_%d_%d" % (j, s), [d])
+        have[(j, s)] = ("wx_%d_%d" % (j, s), ne_on) if j else d
+
+    def place(c):
+        b = 3 + placed.index(c)
+        loc[c] = op("p", mm(PB[b][:], eye, wsrc(c[0], c[1], 0, 512), True, True), [have[c]], b)
+
+    arrived = ["pw0", "pw1"]
     for k in range(R):
         last = k == R - 1
+        stages = [(1 - ci, 0, 512), (ci, 0, 512)] if last else STAGES
+        NS = len(stages)
+        off = [sum(h - l for _, l, h in stages[:i]) // 8 for i in range(NS)]
         for eng in ("s", "v"):
-            for n in ["pu_%d_%d" % (k - 1, i) for i in range(NS)] if k else ["pw0", "pw1"]:
+            for n in arrived:
                 wait(eng, n, npush)
-        ordr = order(k)
-        seq = [(i, n) for i in ordr for n in range(NQ)]
-        for i in ordr:
-            p, w = chunk(i, NQ - 1)
-            nb = w // 128
-            for b in range(nb):
-                mo = op("p", mm(PB[0][:, soff[i] + b:soff[i] + 16 * nb:nb], T.X[:, p + 128 * b:p + 128 * b + 128],
-                                T.ssel[:], True, True), [s_sel] + ev, 0)
+
+        def addin(i, buf, at, sel, deps, stop=False):
+            s, lo, hi = stages[i]
+            nb = (hi - lo) // 128
+            return [op("p", mm(PB[i][:, b:16 * nb:nb], buf[:, at + lo + 128 * b:at + lo + 128 * b + 128], sel, False,
+                               stop and b == nb - 1), deps, i) for b in range(nb)][-1]
+
+        for i, (s, lo, hi) in enumerate(stages):
+            z = op("p", mm(PB[i][:, 0:(hi - lo) // 8], eye, T.zer[:, 0:(hi - lo) // 8], True, False), [c_0, c_eye], i)
+            addin(i, T.X, 512 * theirs(0, s), T.ssel[:], [z, s_sel] + ev)
         if k == 0:
             sc = [xgath("s", a, a + 16) for a in range(0, 64, 16)]
-            done = 0
-            for c in seq:
-                p, w = chunk(*c)
-                wbg[c] = gath("v" if done < 512 * WBV else "s", T.wb[:, p:p + w], T.W[:], T.fl[:, p // 16:(p + w) // 16],
-                              wsc + tails)
-                done += w
+            for n, c in enumerate(WORDER):
+                wgath("v" if n < WBV else "s", *c)
             hs = [hscan(*c) for c in sc]
+            for c in placed:
+                place(c)
         else:
             sc = [xgath("s", a, z) for a, z in ((14, 26), (26, 38), (38, 50), (50, 60), (60, 64))]
             va = xgath("v", 0, 8)
             hs = [hscan(*va), hscan(*sc[0])]
             vb = xgath("v", 8, 14)
             hs += [hscan(*c) for c in [sc[1], vb] + sc[2:]]
-        om = op("s", act(T.old[:], PB[0][:, 0:128]), [mo, hist.get("old")], 0)
+
+        def ewin(j):
+            return T.el[:, 256 * k + 64 * j:256 * k + 64 * j + 64]
+
         e0 = op("v", tt(T.u[:], T.d0[:], T.st[:, 0:4096:64], A.mult), hs + [d0])
-        ee = op("v", tt(T.e[:], T.cnt[:], T.u[:], A.subtract), [e0, dc])
+        ee = op("v", tt(ewin(0), T.cnt[:], T.u[:], A.subtract), [e0, dc])
+        push(ewin(0), "ex_%d" % k, "lr", [ee], [ewin(j) for j in range(1, NQ)])
 
-        def place(c, eng):
-            p, w = chunk(*c)
-            b, o = 2 + at[c] // 512, at[c] % 512
-            o = PB[b][:, o:o + w]
-            loc[c] = op(eng, mm(o, eye, T.wb[:, p:p + w], True, True) if eng == "p" else act(o, T.wb[:, p:p + w]), [wbg[c]], b)
+        def egath(j, s, lo, hi):
+            at = 1024 * j + 512 * s
+            deps = [ee, tl] if j == 0 else [("ex_%d" % k, npush), ("tx", per * len(pairs))]
+            return gath("s", T.eg[:, at + lo:at + hi], ewin(j), rays(j, s, lo, hi), deps)
 
-        egd, bsum, part, pts = {}, {}, {}, {}
-        inp = [c for c in seq if c in at]
-        if k == 0:
-            for c in inp[:PLP]:
-                place(c, "p")
-        for c in inp:
-            if c not in loc:
-                place(c, "s")
-            p, w = chunk(*c)
-            egd[c] = gath("s", T.eg[:, at[c]:at[c] + w], Ew, T.tl[:, p // 16:(p + w) // 16], [ee, tl])
+        def mult(j, s, lo, hi, got):
+            at = 1024 * j + 512 * s
+            out = T.pr[:, at + lo:at + hi]
+            if (j, s) in FUSED:
+                deps = [ee, tl] if j == 0 else [("ex_%d" % k, npush), ("tx", per * len(pairs))]
+                return op("v", tt(out, ewin(j).indirect(rays(j, s, lo, hi)), wsrc(j, s, lo, hi), A.mult), deps + [have[(j, s)]])
+            b = 3 + placed.index((j, s))
+            return op("v", tt(out, T.eg[:, at + lo:at + hi], PB[b][:, lo:hi], A.mult), [got, loc[(j, s)]], b)
 
-        def evac(n):
-            c = seq[n]
-            i, w = c[0], chunk(*c)[1] // 8
-            o = T.snd[:, run[0]:run[0] + w]
-            run[0] += w
-            if c[1] == NQ - 1:
-                d = hist["old"] = op("v", tt(o, PB[n % 2][:, 0:w], T.old[:, soff[i]:soff[i] + w], A.add), [bsum[c], om], n % 2)
-            else:
-                d = op("v", cp(o, PB[n % 2][:, 0:w]), [bsum[c]], n % 2)
-                m = 3 * (128 * k + soff[i]) + c[1] * w
-                send(peers[c[1]], T.lnd[:, m:m + w], o, "rs_%d_%d" % (k, i), [d])
-            part[c] = (o, d)
+        got = {}
+        for c in [(0, s, 0, 512) for s in range(2)] + [(j,) + st for st in stages for j in range(1, NQ)]:
+            if c[:2] not in FUSED:
+                got[c] = egath(*c)
+        for s in (1, 0):
+            pd = mult(0, s, 0, 512, got.get((0, s, 0, 512)))
+            for i in range(NS):
+                if stages[i][0] == s:
+                    addin(i, T.pr, 512 * s, T.ssum[:], [pd, s_sum])
 
-        def chipsum(i):
-            w = chunk(i, 0)[1] // 8
-            m = 128 * k + soff[i]
-            wait("v", "rs_%d_%d" % (k, i), npush)
-            a = op("v", tt(T.t1[:, 0:w], T.lnd[:, 3 * m:3 * m + w], T.lnd[:, 3 * m + w:3 * m + 2 * w], A.add), [hist.get("pt")])
-            o, d = part[(i, NQ - 1)]
-            b = op("v", tt(T.t2[:, 0:w], T.lnd[:, 3 * m + 2 * w:3 * m + 3 * w], o, A.add), [d])
-            hist["pt"] = pts[i] = op("v", tt(T.pt[:, m:m + w], T.t1[:, 0:w], T.t2[:, 0:w], A.add), [a, b])
-            if not last or STAGES[i][0] != ci:
+        full, pts = {}, {}
+
+        def leave(i):
+            s, lo, hi = stages[i]
+            w, m = (hi - lo) // 8, 128 * k + off[i]
+            if not last or s != ci:
+                pts[i] = op("v", cp(T.pt[:, m:m + w], PB[i][:, 0:w]), [full[i]], i)
                 send(partner, T.xs[:, m:m + w], T.pt[:, m:m + w], "xc_%d_%d" % (k, i), [pts[i]])
 
+        for i, (s, lo, hi) in enumerate(stages):
+            for j in range(1, NQ):
+                pd = mult(j, s, lo, hi, got.get((j, s, lo, hi)))
+                full[i] = addin(i, T.pr, 1024 * j + 512 * s, T.ssum[:], [pd], j == NQ - 1)
+                if j == 1 and i:
+                    leave(i - 1)
+        leave(NS - 1)
+
         evs = []
-
-        def newact(i):
-            p, w = chunk(i, NQ - 1)
-            nb, w8, m, r, h = w // 128, w // 8, 128 * k + soff[i], 8 * soff[i], w // 2
-            wait("v", "xc_%d_%d" % (k, i), ne_off)
-            n = op("v", tt(T.rp[:, r:r + w8], T.pt[:, m:m + w8], T.xs[:, m:m + w8], A.add), [pts[i], hist.get(i)])
-            cps, rows, win, lo = [n], 16, T.ysb, p % 512
-            if not last:
-                rows, win, lo = 128, T.X, p
-                for j in range(1, 8):
-                    o, f = T.rp[:, r + w8 * j:r + w8 * j + w8], T.rp[:, r:r + w8]
-                    cps.append(op("v", cp(o, f), [n]) if j < 4 else op("s", act(o, f), [n]))
-                for eng in ("v", "s"):
-                    for b in ["lp_%d_%d" % (k - 1, i)] if k else ["lw0", "lw1"]:
-                        wait(eng, b, ne_on)
-            hb = nb // 2
-            tp = [op("p", mm(PB[b // hb][0:rows, 128 * (b % hb):128 * (b % hb) + 128], T.rp[:, r + b:r + rows * nb:nb], eye,
-                             True, True), cps + [c_eye], b // hb) for b in range(nb)]
-            hist[i] = tp[-1]
-            ab = [op("v", ts(win[0:rows, lo:lo + h], PB[0][0:rows, 0:h], STEP, A.mult, 0.0, A.max), [tp[hb - 1]], 0),
-                  op("s", act(win[0:rows, lo + h:lo + w], PB[1][0:rows, 0:h], AF.Relu, STEP), [tp[-1]], 1)]
-            if last:
-                waits("y", ab)
-                load("y", T.y[:, lo:lo + w], T.ysb[0:16, lo:lo + w], "yo")
-            else:
-                push(T.X[:, p:p + w], "pu_%d_%d" % (k, i), "lp_%d_%d" % (k, i), ab)
-                evs.extend(ab)
-
-        due, todo = {}, list(ordr)
-        for n, c in enumerate(seq):
-            p, w = chunk(*c)
-            out = T.pr[:, p:p + w]
-            if c in at:
-                b, r = 2 + at[c] // 512, at[c] % 512
-                pd = op("v", tt(out, T.eg[:, at[c]:at[c] + w], PB[b][:, r:r + w], A.mult), [egd[c], loc[c]], b)
-            else:
-                pd = op("v", tt(out, Ew.indirect(T.tl[:, p // 16:(p + w) // 16]), T.wb[:, p:p + w], A.mult), [ee, wbg[c], tl])
-            nb = w // 128
-            for b in range(nb):
-                bsum[c] = op("p", mm(PB[n % 2][:, b:16 * nb:nb], T.pr[:, p + 128 * b:p + 128 * b + 128], T.ssum[:], True, True),
-                             [pd, s_sum], n % 2)
-            if n:
-                evac(n - 1)
-            for i in due:
-                due[i] += w
-            if c[1] == NQ - 1:
-                due[c[0]] = 0
-            while todo and due.get(todo[0], -1) >= LAG:
-                chipsum(todo.pop(0))
-        evac(len(seq) - 1)
-        for what, j in TAIL:
-            i = ordr[j]
-            if what == "c" and i in todo:
-                chipsum(i)
-            if what == "n" and (not last or STAGES[i][0] == ci):
-                newact(i)
+        if last:
+            n = op("v", tt(T.rp[:, 0:64], T.xs[:, 128 * k:128 * k + 64], PB[1][:, 0:64], A.add),
+                   [full[1], ("xc_%d_0" % k, ne_off), hist.get("tp")], 1)
+            tp = [op("p", mm(PB[2 * (b // 2)][0:16, 128 * (b % 2):128 * (b % 2) + 128], T.rp[:, b:64:4], eye, True, True),
+                     [n], 2 * (b // 2)) for b in range(4)]
+            ab = [op("v", ts(T.ysb[0:16, 0:256], PB[0][0:16, 0:256], STEP, A.mult, 0.0, A.max), [tp[1]], 0),
+                  op("s", act(T.ysb[0:16, 256:512], PB[2][0:16, 0:256], AF.Relu, STEP), [tp[3]], 2)]
+            waits("y", ab)
+            load("y", T.y[:], T.ysb[0:16, :], "yo")
+            break
+        reps = []
+        for i, (s, lo, hi) in enumerate(stages):
+            w, m, r = (hi - lo) // 8, 128 * k + off[i], 8 * off[i]
+            reps.append(gath("s", T.ptr[:, r:r + 8 * w], T.pt[:, m:m + w], RL[w], [pts[i], rl, hist.get("n")]))
+        for eng in ("v", "s"):
+            for n in ["lp_%d_%d" % (k - 1, i) for i in range(NS)] if k else ["lw0", "lw1"]:
+                wait(eng, n, ne_on)
+        for i, (s, lo, hi) in enumerate(stages):
+            w, m, r, p = (hi - lo) // 8, 128 * k + off[i], 8 * off[i], 512 * theirs(0, s) + lo
+            nb = w // 16
+            n = hist["n"] = op("v", tt(T.rp[:, r:r + 8 * w], T.xs[:, m:m + w].indirect(RL[w]), T.ptr[:, r:r + 8 * w], A.add),
+                               [reps[i], ("xc_%d_%d" % (k, i), ne_off), hist.get("tp")])
+            ab = []
+            for h in range(nb // 2):
+                bank = (i + h) % 3
+                tp = [op("p", mm(PB[bank][:, 128 * b:128 * b + 128], T.rp[:, r + 2 * h + b:r + 8 * w:nb], eye, True, True),
+                         [n], bank) for b in range(2)][-1]
+                o = T.X[:, p + 256 * h:p + 256 * h + 256]
+                if h == 0 and nb > 2:
+                    ab.append(op("v", ts(o, PB[bank][:, 0:256], STEP, A.mult, 0.0, A.max), [tp], bank))
+                else:
+                    ab.append(op("s", act(o, PB[bank][:, 0:256], AF.Relu, STEP), [tp], bank))
+            push(T.X[:, p:p + hi - lo], "pu_%d_%d" % (k, i), "lp_%d_%d" % (k, i), ab)
+            evs.extend(ab)
+        hist["tp"] = tp
         ev = evs
+        arrived = ["pu_%d_%d" % (k, i) for i in range(NS)]
 
     for e in ("v", "s", "p", "q"):
         wait("q", e, cnt[e])

@@ -3,20 +3,38 @@ from concourse.mybir import AluOpType as A, ActivationFunctionType as AF
 
 R = 3
 STEP = 2.0 ** -12
-STAGES = [(1, 0, 256), (1, 256, 512), (0, 0, 512)]
-FUSED = [(0, 1), (1, 1), (1, 0)]
-WORDER = [(2, 1), (3, 1), (2, 0), (3, 0), (1, 1), (1, 0), (0, 0), (0, 1)]
-WBV = 5
-DCH = [("v", 52, 64), ("s", 0, 14), ("s", 14, 28), ("s", 28, 42), ("s", 42, 52)]
+STAGES = [(1, 0, 256), (1, 256, 512), (0, 0, 256), (0, 256, 512)]
+CUTL = [(0, 256), (256, 512)]
+DP = 5
+XP = 8
+SETUP = ["xps dav dbs xw-", "f1s f2v f3s", ""]
+ESPLIT = 0
+XF = 1
+XS = [14, 28, 42, 54, 61, 64]
+XV = [(0, 14), 0, 0, 0, 0, 0]
+WPAIR = [2, 3]
+TURN = [0, 1, 2, 1]
+TURNL = [0, 0, 1, 2]
+PLACED = [(2, 1), (3, 1), (2, 0), (3, 0), (0, 0)]
+WV = [(2, 1), (2, 0), (3, 1), (3, 0)]
+WS = [(1, 1), (0, 1)]
+WS0 = []
+PLACE0 = [(2, 1), (2, 0), (3, 1), (3, 0)]
+XCH0 = [(0, 12), (12, 26), (26, 40), (40, 54), (54, 64)]
+BACK = ("G0 M1 M0 g02 g03 g12 g13 g22 g23 m01 m02 m03 m11 l0v m12 m13 o3 g32 g33 m21 l1v r1s m22 m23 m31 "
+        "l2vd c0f r2s m32 m33 a1 l3v x1sa r3s a2 e00v0 x2sa e01v a3 z00s t012 e02v0 x3sa e03v z01s t031 z02s z03v")
+BACK0 = BACK.replace("G0 M1 M0", "w10s w00s M1 M0") + " p00"
+LAST = "G0 M1 M0 g02 g03 g12 g13 g22 g23 g32 g33 m01 m02 m03 m11 l0v m12 m13 o3 m21 l1v m22 m23 m31 m32 m33 n2 n3 y2s y3v"
+DCH = [("v", 50, 64), ("s", 0, 14), ("s", 14, 28), ("s", 28, 42), ("s", 42, 50)]
 KQ = 0.00012918686694904754
 QUAD = [(1.1219518404595346, 18.754011438386996), (-4.267052247540635, 2.746736091488364),
         (-1.8906565018022652, 14.883958171039492)]
 SCRATCH = {}
-for _n, _w in (("mc", 64), ("dx", 128), ("pdx", 128), ("angf", 4), ("cnt", 64), ("sq", 192), ("rq", 320),
+for _n, _w in (("mc", 64), ("dx", 128), ("pdx", 128), ("fx", 192), ("fd", 192), ("angf", 4), ("cnt", 64), ("sq", 192), ("rq", 320),
                ("rep", 1024), ("ssum", 16), ("ssel", 16), ("fm", 1), ("a64", 64), ("b4i", 4), ("b4", 4), ("kc", 4),
                ("kr", 4), ("pen", 256), ("raw", 256), ("raw2", 256), ("D", 4104), ("X", 4104), ("W", 4104), ("f", 4104),
                ("ind", 1024), ("xg", 4096), ("st", 4096), ("wb", 4096), ("wl", 3072), ("pr", 4096), ("eg", 4096), ("u", 64),
-               ("el", 768), ("pt", 384), ("xs", 384), ("rp", 1024), ("ptr", 1024), ("ysb", 512), ("d0", 64), ("zer", 64),
+               ("el", 768), ("pt", 768), ("xs", 384), ("rp", 1024), ("ptr", 1024), ("rp4", 4096), ("nn", 1024), ("ysb", 512), ("d0", 64), ("zer", 64),
                ("p16", 1), ("rli", 48)):
     SCRATCH[_n] = ("sbuf", [128, _w], "float32")
 for _n, _w in (("angi", 2), ("ipz", 16), ("ipz2", 16), ("ip", 1), ("ip2", 1), ("vc", 256), ("vr", 256), ("col", 256),
@@ -27,10 +45,10 @@ for _n, _w in (("fl", 256), ("tl", 256), ("tll", 192), ("rl", 48)):
 for _n in range(8):
     SCRATCH["bank%d" % _n] = ("psum", [128, 512], "float32")
 SEMAPHORES = (["v", "s", "p", "q", "ldm", "ldx", "lda", "ldc", "yo", "cx", "cd", "lr", "tx"]
-              + ["pd0", "pd1", "pw0", "pw1", "ld0", "ld1", "lw0", "lw1"]
+              + ["cy", "fd", "pd0", "pd1", "pw0", "pw1", "ld0", "ld1", "lw0", "lw1"]
               + ["wx_%d_%d" % (j, s) for j in range(1, 4) for s in range(2)]
-              + ["ex_%d" % k for k in range(R)]
-              + ["%s_%d_%d" % (n, k, s) for n in ("xc", "pu", "lp") for k in range(R) for s in range(len(STAGES))])
+              + ["ex_%d_%d" % (k, j) for k in range(R) for j in range(1, 4)]
+              + ["%s_%d_%d" % (n, k, s) for n in ("xc", "pu", "lp") for k in range(R) for s in range(5)])
 
 
 def ts(out, i, s1, o0, s2=None, o1=None):
@@ -122,11 +140,26 @@ def rank_program(g, core, T, topo):
 
     ids = [DstId(rid=topo.addr(T.cores[r])[0], pnc=topo.addr(T.cores[r])[1]) for r in peers]
 
-    def push(ap, rsem, lsem, deps, dsts=None):
+    off_eng = topo.engines(core, T.cores[partner])
+    LANES = {"a": on_eng, "l": off_eng, "h": [e for e in on_eng if e not in off_eng]}
+    came = {}
+
+    for n in range(4):
+        LANES[n] = on_eng[n * ne_on // 4:(n + 1) * ne_on // 4]
+    other = DstId(rid=topo.addr(T.cores[partner])[0], pnc=topo.addr(T.cores[partner])[1])
+
+    def transfer(to, dsts, src, rsem, lane):
+        return (RemoteDMATransfer(dst_ids=to, dma_engine_mask=sum(1 << e for e in LANES[lane]), remote_sem=T.sem[rsem],
+                                  srcs=[src], dsts=dsts, alu_op=0), len(LANES[lane]))
+
+    def call(transfers, lsem, deps):
         waits("q", deps)
-        g.remote_dma_fused([RemoteDMATransfer(dst_ids=ids, dma_engine_mask=on_mask, remote_sem=T.sem[rsem], srcs=[ap],
-                                              dsts=dsts or [ap] * len(peers), alu_op=0)], local_sem=T.sem[lsem])
-        sent[lsem] = sent.get(lsem, 0) + ne_on
+        g.remote_dma_fused([t for t, _ in transfers], local_sem=T.sem[lsem])
+        sent[lsem] = sent.get(lsem, 0) + sum(n for _, n in transfers)
+
+    def push(ap, rsem, lsem, deps, dsts=None, lane="a", more=()):
+        call(list(more) + [transfer(ids, dsts or [ap] * len(peers), ap, rsem, lane)], lsem, deps)
+        came[rsem] = (rsem, len(LANES[lane]) * len(peers))
 
     PB = [T["bank%d" % i] for i in range(8)]
     eye = T.rep[:, 0:128]
@@ -148,12 +181,32 @@ def rank_program(g, core, T, topo):
     for j in range(1, 8):
         o = T.rep[:, 128 * j:128 * j + 128]
         c_rep.append(op("v", cp(o, eye), [c_eye]) if j < 5 else op("s", act(o, eye), [c_eye]))
-    send(partner, T.pdx[:, 64:128], T.dx[:, 64:128], "cx", [dxl])
+
+    def slot(buf, j):
+        return buf[:, 64 * (j - 1):64 * j]
+
+    if XP:
+        send(partner, T.pdx[:, 64:128], T.dx[:, 64:128], "cx", [dxl])
+    else:
+        push(T.dx[:, 64:128], "cy", "lr", [dxl], [slot(T.fx, j) for j in range(1, NQ)], "h")
+
+    def blk(win, q, h0=0, h1=512):
+        return win[:, 512 * q + h0:512 * q + h1]
+
+    def spread(src, h0, h1, bank, deps):
+        return (h0, h1, bank, [op("p", mm(PB[bank][:, 64 * (h - h0):64 * (h - h0) + 64], T.rep[:, h:1024:8], src, True, True),
+                                  c_rep + list(deps), bank) for h in range(h0, h1)][-1])
+
+    def settle(eng, win, q, m):
+        h0, h1, bank, d = m
+        o, f = blk(win, q, 64 * h0, 64 * h1), PB[bank][:, 0:64 * (h1 - h0)]
+        return op(eng, cp(o, f) if eng == "v" else act(o, f), [d], bank)
+
+    m_x = spread(T.dx[:, 64:128], 0, 8, 0, [dxl])
 
     sq = [T.sq[:, 64 * i:64 * i + 64] for i in range(3)]
     rq = [T.rq[:, 64 * i:64 * i + 64] for i in range(5)]
-    sb = [op("v", ts(sq[i], T.mc[:], QUAD[i][0], A.add), [dm]) for i in range(3)]
-    ss = [op("s", act(sq[i], sq[i], AF.Square), [sb[i]]) for i in range(3)]
+    ss = [op("s", lambda e: e.activation(sq[i], T.mc[:], AF.Square, bias=QUAD[i][0]), [dm]) for i in range(3)]
     r0 = op("v", ts(rq[0], sq[0], QUAD[0][1], A.add, -KQ, A.mult), [ss[0]])
     r1 = op("v", ts(rq[1], sq[1], QUAD[1][1], A.add), [ss[1]])
     r2 = op("v", ts(rq[2], sq[2], QUAD[2][1], A.add), [ss[2]])
@@ -162,21 +215,11 @@ def rank_program(g, core, T, topo):
     r4 = op("v", tt(sq[0], rq[4], rq[3], A.mult), [r0, r3])
     d_c = op("v", ts(T.dx[:, 0:64], sq[0], 1.0, A.add), [r4])
     send(partner, T.pdx[:, 0:64], T.dx[:, 0:64], "cd", [d_c])
+    if not XP:
+        send(partner, T.pdx[:, 64:128], T.dx[:, 64:128], "cx", [dxl])
     c_z = op("q", lambda e: e.iota(T.ipz[:], [[-1, 16]], 0, 1))
-
-    def blk(win, q, h0=0, h1=512):
-        return win[:, 512 * q + h0:512 * q + h1]
-
-    def spread(src, k, deps=()):
-        return [[op("p", mm(PB[2 * k + half][:, 64 * h:64 * h + 64], T.rep[:, 4 * half + h:1024:8], src, True, True),
-                    c_rep + list(deps), 2 * k + half) for h in range(4)][-1] for half in range(2)]
-
-    def settle(win, q, k, m):
-        return [op("v", cp(blk(win, q, 0, 256), PB[2 * k][:, 0:256]), [m[0]], 2 * k),
-                op("s", act(blk(win, q, 256, 512), PB[2 * k + 1][:, 0:256]), [m[1]], 2 * k + 1)]
-
-    m_d = spread(T.dx[:, 0:64], 0, [d_c])
-    m_x = spread(T.dx[:, 64:128], 1, [dxl])
+    ev = [settle("s", T.X, rank, m_x)]
+    m_d = [spread(T.dx[:, 0:64], 0, 4, 1, [d_c]), spread(T.dx[:, 0:64], 4, 8, 2, [d_c])]
 
     a0 = op("v", cp(T.angf[:, 0:2], T.angi[:]), [da])
     a1 = op("v", ts(T.ip2[:], T.ip[:], 15, A.bitwise_and), [c_p])
@@ -185,10 +228,17 @@ def rank_program(g, core, T, topo):
     a4 = op("v", ts(T.b4[:], T.b4i[:], T.fm[:, 0:1], A.add), [a3, c_b])
     a5 = op("v", ts(T.kc[:], T.b4[:], T.angf[:, 2:3], A.mult, 16384.0, A.add), [a4, a2])
     a6 = op("v", ts(T.kr[:], T.b4[:], T.angf[:, 0:1], A.mult, 16384.0, A.add), [a4])
-    e_d = settle(T.D, rank, 0, m_d)
+    e_d = [settle("v", T.D, rank, m_d[0]), settle("s", T.D, rank, m_d[1])]
     push(blk(T.D, rank), "pd0", "ld0", e_d)
-    c_r = [op("q", lambda e: e.iota(T.rli[:, 0:16], [[0, 8], [16, 2]], 0, 0, allow_small_or_imprecise_dtypes=True)),
-           op("q", lambda e: e.iota(T.rli[:, 16:48], [[0, 8], [16, 4]], 0, 0, allow_small_or_imprecise_dtypes=True))]
+
+    def before(j, s):
+        return members[s][(me - j) % NQ]
+
+    widths = sorted({(hi - lo) // 8 for _, lo, hi in STAGES})
+    rat = {w: sum(widths[:n]) // 2 for n, w in enumerate(widths)}
+    c_r = [op("q", lambda e: e.iota(T.rli[:, rat[w]:rat[w] + w // 2], [[0, 8], [16, w // 16]], 0, 0,
+                                    allow_small_or_imprecise_dtypes=True)) for w in widths]
+    nr = sum(widths) // 2
     for k in range(4):
         lc = op("v", ts(T.vc[:, k:256:4], T.a64[:], T.angf[:, 0:1], A.mult, T.kc[:, k:k + 1], A.add), [a5, c_a])
         lr = op("v", ts(T.vr[:, k:256:4], T.a64[:], T.angf[:, 1:2], A.mult, T.kr[:, k:k + 1], A.add), [a6, c_a])
@@ -196,63 +246,87 @@ def rank_program(g, core, T, topo):
     c2 = op("v", ts(T.row[:], T.vr[:], 3, A.logical_shift_right, 0x1FFFFFC0, A.bitwise_and), [lr])
     c3 = op("v", ts(T.pen[:], T.col[:], 64.0, A.is_ge, 4096.0, A.mult), [c1])
     c4 = op("v", tt(T.raw[:], T.col[:], T.row[:], A.add), [c1, c2])
-    wait("p", "cd", ne_off)
-    m_dp = spread(T.pdx[:, 0:64], 2)
-    wait("p", "cx", ne_off)
-    m_xp = spread(T.pdx[:, 64:128], 3)
-    e_dp = settle(T.D, partner, 2, m_dp)
-    push(blk(T.D, partner), "pd1", "ld1", e_dp)
-    e_d += e_dp
-    e_x = settle(T.X, rank, 1, m_x)
-    push(blk(T.X, rank), "pw0", "lw0", e_x)
-    e_xp = settle(T.X, partner, 3, m_xp)
-    push(blk(T.X, partner), "pw1", "lw1", e_xp)
-    ev = e_x + e_xp
     c6 = op("v", tt(T.raw2[:], T.raw[:], T.pen[:], A.add), [c3, c4])
     fl = op("v", ts(T.fl[:], T.raw2[:], 4096.0, A.min), [c6])
+    cd = ("cd", ne_off)
+    if DP < 8:
+        push(T.pdx[:, 0:64], "fd", "lr", [cd], [slot(T.fd, j) for j in range(1, NQ)])
+    arrived = ["pw1", "pw0"] if XP else ["pw1"]
+    banks = [3]
+
+    def setup(steps):
+        for step in steps.split():
+            banks[0] = (banks[0] + 1) % 8
+            what, eng, b = step[0:2], step[2], banks[0]
+            if what == "da":
+                e_d.append(settle(eng, T.D, partner, spread(T.pdx[:, 0:64], 0, DP, b, [cd])))
+                push(blk(T.D, partner, 0, 64 * DP), "pd1", "ld1", e_d[-1:])
+                if XP and not XF:
+                    push(blk(T.X, rank), "pw0", "lw0", ev)
+            elif what == "db":
+                e_d.append(settle(eng, T.D, partner, spread(T.pdx[:, 0:64], DP, 8, b, [cd])))
+            elif what == "xp":
+                ev.append(settle(eng, T.X, partner, spread(T.pdx[:, 64:128], 0, 8, b, [("cx", ne_off)])))
+                xp = ev[-1]
+            elif what == "xw":
+                if XF:
+                    push(blk(T.X, partner), "pw1", "lw1", ev, None, "h",
+                         [transfer(ids, [blk(T.X, rank)] * len(peers), blk(T.X, rank), "pw1", "l")])
+                    came["pw0"] = came["pw1"] = ("pw1", npush)
+                else:
+                    push(blk(T.X, partner), "pw1", "lw1", ev)
+            elif what[0] == "f":
+                j = int(what[1])
+                e_d.append(settle(eng, T.D, before(j, 1 - ci), spread(slot(T.fd, j), DP, 8, b, [came["fd"]])))
+            else:
+                j = int(what[1])
+                ev.append(settle(eng, T.X, before(j, ci), spread(slot(T.fx, j), 0, 8, b, [came["cy"]])))
+
+    setup(SETUP[0])
     in0 = op("v", ms(T.ind[:], 0.0))
     in1 = op("v", ms(T.ind[:, 0:1024:64], 1.0), [in0])
     c5 = op("v", ts(T.tp[:], T.vr[:], 9, A.arith_shift_right), [lr])
-    tl = op("v", ts(T.tl[:], T.tp[:], 0.0, A.max, 63.0, A.min), [c5])
     s_1 = op("v", ts(T.ipz2[:], T.ipz[:], 15, A.bitwise_and), [c_z])
     s_sel = op("v", ts(T.ssel[:], T.ipz[:], 0.0, A.is_equal, 2048.0, A.mult), [c_z])
     s_sum = op("v", ts(T.ssum[:], T.ipz2[:], 0.0, A.is_equal), [s_1])
     p16 = op("v", cp(T.p16[:], T.ip2[:]), [a1])
-    rl = op("v", ts(T.rl[:], T.rli[:], T.p16[:, 0:1], A.add), c_r + [p16])
-    RL = {32: T.rl[:, 0:16], 64: T.rl[:, 16:48]}
+    rl = op("v", ts(T.rl[:, 0:nr], T.rli[:, 0:nr], T.p16[:, 0:1], A.add), c_r + [p16])
+    RL = {w: T.rl[:, rat[w]:rat[w] + w // 2] for w in widths}
 
     def theirs(j, s):
         return members[s][(me + j) % NQ]
 
     def wsrc(j, s, lo, hi):
-        return blk(T.wb, theirs(0, s), lo, hi) if j == 0 else blk(T.wl, 2 * (j - 1) + s, lo, hi)
+        return blk(T.wb, s, lo, hi) if j == 0 else blk(T.wl, 2 * (j - 1) + s, lo, hi)
 
     def rays(j, s, lo, hi):
-        t, b = (T.tl, theirs(0, s)) if j == 0 else (T.tll, 2 * (j - 1) + s)
+        t, b = (T.tl, s) if j == 0 else (T.tll, 2 * (j - 1) + s)
         return t[:, 32 * b + lo // 16:32 * b + hi // 16]
 
-    waits("q", [tl])
-    pairs = [(j, s) for j in range(1, NQ) for s in range(2)]
-    per = ne_on // 8
-    g.remote_dma_fused([RemoteDMATransfer(
-        dst_ids=[ids[j - 1]], dma_engine_mask=sum(1 << e for e in on_eng[per * n:per * n + per]), remote_sem=T.sem.tx,
-        srcs=[T.tl[:, 32 * theirs(j, s):32 * theirs(j, s) + 32]], dsts=[rays(j, s, 0, 512)], alu_op=0)
-        for n, (j, s) in enumerate(pairs)], local_sem=T.sem.lr)
-    sent["lr"] += per * len(pairs)
+    for j in range(NQ):
+        for s in range(2):
+            o, b = 64 * j + 32 * s, 32 * theirs(j, s)
+            tl = op("v", ts(T.tl[:, o:o + 32], T.tp[:, b:b + 32], 0.0, A.max, 63.0, A.min), [c5])
+    call([transfer([ids[j - 1]], [T.tll[:, 64 * j - 64:64 * j]], T.tl[:, 64 * j:64 * j + 64], "tx", j) for j in range(1, NQ)],
+         "lr", [tl])
+    tx = ("tx", sum(len(LANES[j]) for j in range(1, NQ)))
 
     def gath(eng, out, win, off, deps):
         src = win.indirect(off)
         return op(eng, cp(out, src) if eng == "v" else act(out, src), deps)
 
+    setup(SETUP[1])
     for eng in ("s", "v"):
         wait(eng, "pd0", npush)
         wait(eng, "pd1", npush)
 
     dg = {a: gath(eng, T.f[:, 64 * a:64 * z], T.D[:], T.fl[:, 4 * a:4 * z], [fl] + e_d + tails) for eng, a, z in DCH}
     wsc = []
-    for eng, a, z in DCH:
+    for n, (eng, a, z) in enumerate(DCH):
         wsc.append(op("v", scan(T.W[:, 64 * a:64 * z], T.ind[:, 0:64 * (z - a)], T.f[:, 64 * a:64 * z], A.max, A.mult),
                       [dg[a], in1]))
+        if n == 0:
+            setup(SETUP[2])
     d0 = op("v", cp(T.d0[:], T.f[:, 0:4096:64]), wsc)
     fz = op("v", ms(T.f[:, 0:4096:64], 0.0), [d0])
 
@@ -263,137 +337,185 @@ def rank_program(g, core, T, topo):
         lo = 64 * a - 1 if a else None
         return op("v", scan(T.st[:, 64 * z - 1:lo:-1], T.f[:, 64 * z:64 * a:-1], T.xg[:, 64 * z - 1:lo:-1]), [dep, fz])
 
-    placed = [c for c in WORDER if c not in FUSED]
     have, loc = {}, {}
 
     def wgath(eng, j, s):
         b = theirs(j, s)
-        d = gath(eng, blk(T.wb, b), T.W[:], T.fl[:, 32 * b:32 * b + 32], wsc + tails)
-        if j:
-            send(peers[j - 1], wsrc(j, s, 0, 512), blk(T.wb, b), "wx_%d_%d" % (j, s), [d])
-        have[(j, s)] = ("wx_%d_%d" % (j, s), ne_on) if j else d
+        d = have[(j, s)] = gath(eng, blk(T.wb, 2 * j + s), T.W[:], T.fl[:, 32 * b:32 * b + 32], wsc + tails)
+        if j in WPAIR:
+            if (j, 1 - s) in have:
+                send(peers[j - 1], T.wl[:, 1024 * j - 1024:1024 * j], T.wb[:, 1024 * j:1024 * j + 1024], "wx_%d_0" % j,
+                     [d, have[(j, 1 - s)]])
+                have[(j, 0)] = have[(j, 1)] = ("wx_%d_0" % j, ne_on)
+        elif j:
+            send(peers[j - 1], wsrc(j, s, 0, 512), blk(T.wb, 2 * j + s), "wx_%d_%d" % (j, s), [d])
+            have[(j, s)] = ("wx_%d_%d" % (j, s), ne_on)
 
     def place(c):
-        b = 3 + placed.index(c)
+        b = 3 + PLACED.index(c)
         loc[c] = op("p", mm(PB[b][:], eye, wsrc(c[0], c[1], 0, 512), True, True), [have[c]], b)
 
-    arrived = ["pw0", "pw1"]
     for k in range(R):
         last = k == R - 1
-        stages = [(1 - ci, 0, 512), (ci, 0, 512)] if last else STAGES
+        stages = [(s, lo, hi) for s in (1 - ci, ci) for lo, hi in CUTL] if last else STAGES
         NS = len(stages)
-        off = [sum(h - l for _, l, h in stages[:i]) // 8 for i in range(NS)]
-        for eng in ("s", "v"):
-            for n in arrived:
-                wait(eng, n, npush)
+        wid = [(h - l) // 8 for _, l, h in stages]
+        off = [sum(wid[:i]) for i in range(NS)]
+        for eng in ("s", "v") if k else ():
+            waits(eng, [came[n] for n in arrived])
 
-        def addin(i, buf, at, sel, deps, stop=False):
+        def addin(i, buf, at, sel, deps, stop=False, early=False):
             s, lo, hi = stages[i]
             nb = (hi - lo) // 128
-            return [op("p", mm(PB[i][:, b:16 * nb:nb], buf[:, at + lo + 128 * b:at + lo + 128 * b + 128], sel, False,
-                               stop and b == nb - 1), deps, i) for b in range(nb)][-1]
+            o = wid[i - 3] if early and i >= 3 else 0
+            return [op("p", mm(PB[i % 3][:, o + b:o + 16 * nb:nb], buf[:, at + lo + 128 * b:at + lo + 128 * b + 128], sel, False,
+                               stop and b == nb - 1), deps, i % 3) for b in range(nb)][-1]
 
-        for i, (s, lo, hi) in enumerate(stages):
-            z = op("p", mm(PB[i][:, 0:(hi - lo) // 8], eye, T.zer[:, 0:(hi - lo) // 8], True, False), [c_0, c_eye], i)
-            addin(i, T.X, 512 * theirs(0, s), T.ssel[:], [z, s_sel] + ev)
+        both = [wid[i] + (wid[i + 3] if i + 3 < NS else 0) for i in range(NS)]
+        zs = [op("p", mm(PB[i][:, 0:both[i]], eye, T.zer[:, 0:both[i]], True, False), [c_0, c_eye], i) for i in range(3)]
+        for i in range(NS):
+            addin(i, T.X, 512 * theirs(0, stages[i][0]), T.ssel[:], [zs[i % 3], s_sel] + ev, early=True)
         if k == 0:
-            sc = [xgath("s", a, a + 16) for a in range(0, 64, 16)]
-            for n, c in enumerate(WORDER):
-                wgath("v" if n < WBV else "s", *c)
+            for n, c in enumerate(WV):
+                wgath("s" if n in WS0 else "v", *c)
+            waits("s", [came[n] for n in arrived])
+            sc = [xgath("s", a, z) for a, z in XCH0]
+            for c in WS:
+                wgath("s", *c)
             hs = [hscan(*c) for c in sc]
-            for c in placed:
+            for c in PLACE0:
                 place(c)
         else:
-            sc = [xgath("s", a, z) for a, z in ((14, 26), (26, 38), (38, 50), (50, 60), (60, 64))]
-            va = xgath("v", 0, 8)
-            hs = [hscan(*va), hscan(*sc[0])]
-            vb = xgath("v", 8, 14)
-            hs += [hscan(*c) for c in [sc[1], vb] + sc[2:]]
+            sc = [xgath("s", a, z) for a, z in zip(XS, XS[1:])]
+            hs = []
+            for c in XV:
+                hs.append(hscan(*(xgath("v", *c) if c else sc.pop(0))))
 
         def ewin(j):
             return T.el[:, 256 * k + 64 * j:256 * k + 64 * j + 64]
 
         e0 = op("v", tt(T.u[:], T.d0[:], T.st[:, 0:4096:64], A.mult), hs + [d0])
         ee = op("v", tt(ewin(0), T.cnt[:], T.u[:], A.subtract), [e0, dc])
-        push(ewin(0), "ex_%d" % k, "lr", [ee], [ewin(j) for j in range(1, NQ)])
+        if ESPLIT:
+            for j in range(1, NQ):
+                send(peers[j - 1], ewin(j), ewin(0), "ex_%d_%d" % (k, j), [ee])
+            ex = {j: ("ex_%d_%d" % (k, j), ne_on) for j in range(1, NQ)}
+        else:
+            push(ewin(0), "ex_%d_1" % k, "lr", [ee], [ewin(j) for j in range(1, NQ)])
+            ex = {j: ("ex_%d_1" % k, npush) for j in range(1, NQ)}
 
         def egath(j, s, lo, hi):
             at = 1024 * j + 512 * s
-            deps = [ee, tl] if j == 0 else [("ex_%d" % k, npush), ("tx", per * len(pairs))]
+            deps = [ee, tl] if j == 0 else [ex[j], tx]
             return gath("s", T.eg[:, at + lo:at + hi], ewin(j), rays(j, s, lo, hi), deps)
 
         def mult(j, s, lo, hi, got):
             at = 1024 * j + 512 * s
             out = T.pr[:, at + lo:at + hi]
-            if (j, s) in FUSED:
-                deps = [ee, tl] if j == 0 else [("ex_%d" % k, npush), ("tx", per * len(pairs))]
+            if got is None:
+                deps = [ee, tl] if j == 0 else [ex[j], tx]
                 return op("v", tt(out, ewin(j).indirect(rays(j, s, lo, hi)), wsrc(j, s, lo, hi), A.mult), deps + [have[(j, s)]])
-            b = 3 + placed.index((j, s))
+            b = 3 + PLACED.index((j, s))
             return op("v", tt(out, T.eg[:, at + lo:at + hi], PB[b][:, lo:hi], A.mult), [got, loc[(j, s)]], b)
 
-        got = {}
-        for c in [(0, s, 0, 512) for s in range(2)] + [(j,) + st for st in stages for j in range(1, NQ)]:
-            if c[:2] not in FUSED:
-                got[c] = egath(*c)
-        for s in (1, 0):
-            pd = mult(0, s, 0, 512, got.get((0, s, 0, 512)))
-            for i in range(NS):
-                if stages[i][0] == s:
-                    addin(i, T.pr, 512 * s, T.ssum[:], [pd, s_sum])
+        got, own, full, pts, reps, turned, news, evs = {}, {}, {}, {}, {}, {}, {}, []
 
-        full, pts = {}, {}
+        def relu(eng, out, in_, deps, bank):
+            return op(eng, ts(out, in_, STEP, A.mult, 0.0, A.max) if eng == "v" else act(out, in_, AF.Relu, STEP), deps, bank)
 
-        def leave(i):
+        for step in (BACK0 if k == 0 else LAST if last else BACK).split():
+            what, i = step[0], int(step[1])
+            if what == "w":
+                wgath(step[3], i, int(step[2]))
+                continue
+            if what == "p":
+                place((i, int(step[2])))
+                continue
+            if what == "G":
+                got[(0, i)] = egath(0, i, 0, 512)
+                continue
+            if what == "M":
+                own[i] = mult(0, i, 0, 512, got.get((0, i)))
+                for n in range(NS):
+                    if stages[n][0] == i:
+                        addin(n, T.pr, 512 * i, T.ssum[:], [own[i], s_sum], early=True)
+                continue
             s, lo, hi = stages[i]
-            w, m = (hi - lo) // 8, 128 * k + off[i]
-            if not last or s != ci:
-                pts[i] = op("v", cp(T.pt[:, m:m + w], PB[i][:, 0:w]), [full[i]], i)
-                send(partner, T.xs[:, m:m + w], T.pt[:, m:m + w], "xc_%d_%d" % (k, i), [pts[i]])
-
-        for i, (s, lo, hi) in enumerate(stages):
-            for j in range(1, NQ):
-                pd = mult(j, s, lo, hi, got.get((j, s, lo, hi)))
+            w, m, r, p, nb = wid[i], 128 * k + off[i], 8 * off[i], 512 * theirs(0, s) + lo, (hi - lo) // 128
+            mp = 256 * k + sum(both[:i])
+            acc, bank = PB[i % 3][:, 0:w], (TURNL if last else TURN)[i]
+            if what == "g":
+                got[step[1:]] = egath(int(step[2]), s, lo, hi)
+            elif what == "m":
+                j = int(step[2])
+                pd = mult(j, s, lo, hi, got.get(step[1:]))
                 full[i] = addin(i, T.pr, 1024 * j + 512 * s, T.ssum[:], [pd], j == NQ - 1)
-                if j == 1 and i:
-                    leave(i - 1)
-        leave(NS - 1)
-
-        evs = []
+            elif what == "o":
+                at = 256 * k + sum(both[:i - 3]) + wid[i - 3]
+                wait("p", *op("p", mm(acc, eye, T.pt[:, at:at + w], True, False), [pts[i - 3]], i % 3))
+            elif what == "l":
+                o, f = T.pt[:, mp:mp + both[i]], PB[i % 3][:, 0:both[i]]
+                pts[i] = op(step[2], cp(o, f) if step[2] == "v" else act(o, f), [full[i]], i % 3)
+                held = (T.xs[:, m:m + w], T.pt[:, mp:mp + w], "xc_%d_%d" % (k, i), [pts[i]])
+                if len(step) == 3:
+                    send(partner, *held)
+            elif what == "r":
+                reps[i] = gath(step[2], T.ptr[:, r:r + 8 * w], T.pt[:, mp:mp + w], RL[w], [pts[i], rl, hist.get("n")])
+            elif what == "a":
+                n = hist["n"] = op("v", tt(T.rp[:, r:r + 8 * w], T.xs[:, m:m + w].indirect(RL[w]), T.ptr[:, r:r + 8 * w], A.add),
+                                   [reps[i], ("xc_%d_%d" % (k, i), ne_off), hist.get(i)])
+                hist[i] = turned[i] = [op("p", mm(PB[bank][:, 128 * b:128 * b + 128], T.rp[:, r + b:r + 8 * w:nb], eye, True, True),
+                                          [n], bank) for b in range(nb)][-1]
+            elif what == "x":
+                left = "lp_%d_%d" % (k - 1, i) if k else "lw%d" % (s != ci or XF)
+                wait(step[2], left, sent.get(left, 0))
+                d = relu(step[2], T.X[:, p:p + hi - lo], PB[bank][:, 0:hi - lo], [turned[i]], bank)
+                push(T.X[:, p:p + hi - lo], "pu_%d_%d" % (k, i), "lp_%d_%d" % (k, i), [d], lane=step[3])
+                evs.append(d)
+            elif what == "c":
+                def nn(j, at=512 * k + off[i], w=w):
+                    return T.nn[:, at + 128 * j:at + 128 * j + w]
+                news[i] = nn
+                d = reps[i] = op("v", tt(nn(0), T.pt[:, mp:mp + w], T.xs[:, m:m + w], A.add), [pts[i], ("xc_%d_%d" % (k, i), ne_off)])
+                if step[2] == "b":
+                    two = [T.nn[:, 512 * k + 128 * j + off[i - 1]:512 * k + 128 * j + off[i] + w] for j in range(NQ)]
+                    push(two[0], "pu_%d_%d" % (k, i), "lr", [d], two[1:])
+                    came["pu_%d_%d" % (k, i - 1)] = came["pu_%d_%d" % (k, i)]
+                elif step[2] == "f":
+                    push(nn(0), "pu_%d_%d" % (k, i), "lr", [d] + held[3], [nn(j) for j in range(1, NQ)], "h",
+                         [transfer([other], [held[0]], held[1], held[2], "l")])
+                elif step[2] == "a":
+                    push(nn(0), "pu_%d_%d" % (k, i), "lr", [d], [nn(j) for j in range(1, NQ)])
+            elif what == "e":
+                j = int(step[2])
+                at = 4 * r + 8 * w * j
+                reps[(i, j)] = gath(step[3], T.rp4[:, at:at + 8 * w], news[i](j), RL[w],
+                                    [rl, came["pu_%d_%d" % (k, i)] if j else reps[i], hist.get((i, j))])
+            if what == "t" or what == "e" and len(step) == 5:
+                j, bank = int(step[2]), int(step[-1])
+                at = 4 * r + 8 * w * j
+                hist[(i, j)] = [op("p", mm(PB[bank][:, 128 * b:128 * b + 128], T.rp4[:, at + b:at + 8 * w:nb], eye, True, True),
+                                   [reps[(i, j)]], bank) for b in range(nb)][-1]
+                turned[(i, j)] = bank
+            elif what == "z":
+                j = int(step[2])
+                bank, p = turned[(i, j)], 512 * theirs(-j, s) + lo
+                if k == 0 and j == 0:
+                    wait(step[3], "lw%d" % (s != ci or XF), sent.get("lw%d" % (s != ci or XF), 0))
+                evs.append(relu(step[3], T.X[:, p:p + hi - lo], PB[bank][:, 0:hi - lo], [hist[(i, j)]], bank))
+            elif what == "n":
+                h = i - NS // 2
+                mo = 128 * k + off[h]
+                n = op("v", tt(T.rp[:, off[h]:off[h] + w], T.xs[:, mo:mo + w], acc, A.add),
+                       [full[i], ("xc_%d_%d" % (k, h), ne_off), hist.get(0)], i % 3)
+                tp = [op("p", mm(PB[bank][0:16, 128 * b:128 * b + 128], T.rp[:, off[h] + b:off[h] + w:nb], eye, True, True),
+                         [n], bank) for b in range(nb)][-1]
+                turned[i] = tp
+            elif what == "y":
+                evs.append(relu(step[2], T.ysb[0:16, lo:hi], PB[bank][0:16, 0:hi - lo], [turned[i]], bank))
         if last:
-            n = op("v", tt(T.rp[:, 0:64], T.xs[:, 128 * k:128 * k + 64], PB[1][:, 0:64], A.add),
-                   [full[1], ("xc_%d_0" % k, ne_off), hist.get("tp")], 1)
-            tp = [op("p", mm(PB[2 * (b // 2)][0:16, 128 * (b % 2):128 * (b % 2) + 128], T.rp[:, b:64:4], eye, True, True),
-                     [n], 2 * (b // 2)) for b in range(4)]
-            ab = [op("v", ts(T.ysb[0:16, 0:256], PB[0][0:16, 0:256], STEP, A.mult, 0.0, A.max), [tp[1]], 0),
-                  op("s", act(T.ysb[0:16, 256:512], PB[2][0:16, 0:256], AF.Relu, STEP), [tp[3]], 2)]
-            waits("y", ab)
+            waits("y", evs)
             load("y", T.y[:], T.ysb[0:16, :], "yo")
-            break
-        reps = []
-        for i, (s, lo, hi) in enumerate(stages):
-            w, m, r = (hi - lo) // 8, 128 * k + off[i], 8 * off[i]
-            reps.append(gath("s", T.ptr[:, r:r + 8 * w], T.pt[:, m:m + w], RL[w], [pts[i], rl, hist.get("n")]))
-        for eng in ("v", "s"):
-            for n in ["lp_%d_%d" % (k - 1, i) for i in range(NS)] if k else ["lw0", "lw1"]:
-                wait(eng, n, ne_on)
-        for i, (s, lo, hi) in enumerate(stages):
-            w, m, r, p = (hi - lo) // 8, 128 * k + off[i], 8 * off[i], 512 * theirs(0, s) + lo
-            nb = w // 16
-            n = hist["n"] = op("v", tt(T.rp[:, r:r + 8 * w], T.xs[:, m:m + w].indirect(RL[w]), T.ptr[:, r:r + 8 * w], A.add),
-                               [reps[i], ("xc_%d_%d" % (k, i), ne_off), hist.get("tp")])
-            ab = []
-            for h in range(nb // 2):
-                bank = (i + h) % 3
-                tp = [op("p", mm(PB[bank][:, 128 * b:128 * b + 128], T.rp[:, r + 2 * h + b:r + 8 * w:nb], eye, True, True),
-                         [n], bank) for b in range(2)][-1]
-                o = T.X[:, p + 256 * h:p + 256 * h + 256]
-                if h == 0 and nb > 2:
-                    ab.append(op("v", ts(o, PB[bank][:, 0:256], STEP, A.mult, 0.0, A.max), [tp], bank))
-                else:
-                    ab.append(op("s", act(o, PB[bank][:, 0:256], AF.Relu, STEP), [tp], bank))
-            push(T.X[:, p:p + hi - lo], "pu_%d_%d" % (k, i), "lp_%d_%d" % (k, i), ab)
-            evs.extend(ab)
-        hist["tp"] = tp
         ev = evs
         arrived = ["pu_%d_%d" % (k, i) for i in range(NS)]
 

from concourse.bass import DstId, RemoteDMATransfer
from concourse.mybir import AluOpType as A, ActivationFunctionType as AF

R = 3
STEP = 2.0 ** -12
STAGES = [(1, 0, 256), (1, 256, 512), (0, 0, 256), (0, 256, 512)]
CUTL = [(0, 256), (256, 512)]
DP = 5
XP = 8
SETUP = ["xps dav dbs xw-", "f1s f2v f3s", ""]
ESPLIT = 0
XF = 1
XS = [14, 28, 42, 54, 61, 64]
XV = [(0, 14), 0, 0, 0, 0, 0]
WPAIR = [2, 3]
TURN = [0, 1, 2, 1]
TURNL = [0, 0, 1, 2]
PLACED = [(2, 1), (3, 1), (2, 0), (3, 0), (0, 0)]
WV = [(2, 1), (2, 0), (3, 1), (3, 0)]
WS = [(1, 1), (0, 1)]
WS0 = []
PLACE0 = [(2, 1), (2, 0), (3, 1), (3, 0)]
XCH0 = [(0, 12), (12, 26), (26, 40), (40, 54), (54, 64)]
BACK = ("G0 M1 M0 g02 g03 g12 g13 g22 g23 m01 m02 m03 m11 l0v m12 m13 o3 g32 g33 m21 l1v r1s m22 m23 m31 "
        "l2vd c0f r2s m32 m33 a1 l3v x1sa r3s a2 e00v0 x2sa e01v a3 z00s t012 e02v0 x3sa e03v z01s t031 z02s z03v")
BACK0 = BACK.replace("G0 M1 M0", "w10s w00s M1 M0") + " p00"
LAST = "G0 M1 M0 g02 g03 g12 g13 g22 g23 g32 g33 m01 m02 m03 m11 l0v m12 m13 o3 m21 l1v m22 m23 m31 m32 m33 n2 n3 y2s y3v"
DCH = [("v", 50, 64), ("s", 0, 14), ("s", 14, 28), ("s", 28, 42), ("s", 42, 50)]
KQ = 0.00012918686694904754
QUAD = [(1.1219518404595346, 18.754011438386996), (-4.267052247540635, 2.746736091488364),
        (-1.8906565018022652, 14.883958171039492)]
SCRATCH = {}
for _n, _w in (("mc", 64), ("dx", 128), ("pdx", 128), ("fx", 192), ("fd", 192), ("angf", 4), ("cnt", 64), ("sq", 192), ("rq", 320),
               ("rep", 1024), ("ssum", 16), ("ssel", 16), ("fm", 1), ("a64", 64), ("b4i", 4), ("b4", 4), ("kc", 4),
               ("kr", 4), ("pen", 256), ("raw", 256), ("raw2", 256), ("D", 4104), ("X", 4104), ("W", 4104), ("f", 4104),
               ("ind", 1024), ("xg", 4096), ("st", 4096), ("wb", 4096), ("wl", 3072), ("pr", 4096), ("eg", 4096), ("u", 64),
               ("el", 768), ("pt", 768), ("xs", 384), ("rp", 1024), ("ptr", 1024), ("rp4", 4096), ("nn", 1024), ("ysb", 512), ("d0", 64), ("zer", 64),
               ("p16", 1), ("rli", 48)):
    SCRATCH[_n] = ("sbuf", [128, _w], "float32")
for _n, _w in (("angi", 2), ("ipz", 16), ("ipz2", 16), ("ip", 1), ("ip2", 1), ("vc", 256), ("vr", 256), ("col", 256),
               ("row", 256), ("tp", 256)):
    SCRATCH[_n] = ("sbuf", [128, _w], "int32")
for _n, _w in (("fl", 256), ("tl", 256), ("tll", 192), ("rl", 48)):
    SCRATCH[_n] = ("sbuf", [128, _w], "uint16")
for _n in range(8):
    SCRATCH["bank%d" % _n] = ("psum", [128, 512], "float32")
SEMAPHORES = (["v", "s", "p", "q", "ldm", "ldx", "lda", "ldc", "yo", "cx", "cd", "lr", "tx"]
              + ["cy", "fd", "pd0", "pd1", "pw0", "pw1", "ld0", "ld1", "lw0", "lw1"]
              + ["wx_%d_%d" % (j, s) for j in range(1, 4) for s in range(2)]
              + ["ex_%d_%d" % (k, j) for k in range(R) for j in range(1, 4)]
              + ["%s_%d_%d" % (n, k, s) for n in ("xc", "pu", "lp") for k in range(R) for s in range(5)])


def ts(out, i, s1, o0, s2=None, o1=None):
    if o1 is None:
        return lambda e: e.tensor_scalar(out, i, s1, None, o0)
    return lambda e: e.tensor_scalar(out, i, s1, s2, o0, o1)


def tt(out, a, b, o):
    return lambda e: e.tensor_tensor(out, a, b, o)


def cp(out, i):
    return lambda e: e.tensor_copy(out, i)


def act(out, i, fn=AF.Copy, scale=1.0):
    return lambda e: e.activation(out, i, fn, scale=scale)


def mm(out, l, r, a, z):
    return lambda e: e.matmul(out, l, r, a, z)


def ms(ap, c):
    return lambda e: e.memset(ap, c)


def scan(out, d0, d1, o0=A.mult, o1=A.add):
    return lambda e: e.tensor_tensor_scan(out, d0, d1, 0.0, o0, o1)


def rank_program(g, core, T, topo):
    rank = T.rank_of(core)
    if rank is None:
        return
    chips = []
    for c in T.cores:
        if topo.chip(c) not in chips:
            chips.append(topo.chip(c))
    members = [[r for r, c in enumerate(T.cores) if topo.chip(c) == ch] for ch in chips]
    ci = chips.index(topo.chip(core))
    mine = members[ci]
    me = mine.index(rank)
    NQ = len(mine)
    partner = members[1 - ci][me]
    peers = [mine[(me + k) % NQ] for k in range(1, NQ)]
    on_mask = topo.mask(core, T.cores[peers[0]])
    on_eng = topo.engines(core, T.cores[peers[0]])
    ne_on = len(on_eng)
    ne_off = len(topo.engines(core, T.cores[partner]))
    npush = ne_on * (NQ - 1)

    ENG = {"v": g.vector, "s": g.scalar, "p": g.tensor, "q": g, "y": g.sync}
    cnt, known, touch, sent, hist = {}, {}, {}, {}, {}

    def wait(eng, sem, val):
        if known.get((eng, sem), 0) < val:
            ENG[eng].wait_ge(T.sem[sem], val)
            known[(eng, sem)] = val

    def waits(eng, deps):
        for d in deps:
            if d is not None:
                wait(eng, d[0], d[1])

    def op(eng, fn, deps=(), bank=None):
        waits(eng, deps)
        use = touch.setdefault(bank, {}) if bank is not None else {}
        for (o, n) in use.items():
            if o != eng:
                wait(eng, o, n)
        fn(ENG[eng]).then_inc(T.sem[eng], 1)
        cnt[eng] = cnt.get(eng, 0) + 1
        use[eng] = cnt[eng]
        return (eng, cnt[eng])

    def load(eng, out, in_, sem):
        ENG[eng].dma_start(out, in_).then_inc(T.sem[sem], 16)
        hist[sem] = hist.get(sem, 0) + 16
        return (sem, hist[sem])

    def send(dst, out, in_, rsem, deps):
        waits("q", deps)
        c = T.cores[dst]
        rid, pid, _ = topo.addr(c)
        g.remote_dma(out, in_, T.sem[rsem], T.sem.lr, pid, rid, topo.mask(core, c))
        sent["lr"] = sent.get("lr", 0) + len(topo.engines(core, c))

    ids = [DstId(rid=topo.addr(T.cores[r])[0], pnc=topo.addr(T.cores[r])[1]) for r in peers]

    off_eng = topo.engines(core, T.cores[partner])
    LANES = {"a": on_eng, "l": off_eng, "h": [e for e in on_eng if e not in off_eng]}
    came = {}

    for n in range(4):
        LANES[n] = on_eng[n * ne_on // 4:(n + 1) * ne_on // 4]
    other = DstId(rid=topo.addr(T.cores[partner])[0], pnc=topo.addr(T.cores[partner])[1])

    def transfer(to, dsts, src, rsem, lane):
        return (RemoteDMATransfer(dst_ids=to, dma_engine_mask=sum(1 << e for e in LANES[lane]), remote_sem=T.sem[rsem],
                                  srcs=[src], dsts=dsts, alu_op=0), len(LANES[lane]))

    def call(transfers, lsem, deps):
        waits("q", deps)
        g.remote_dma_fused([t for t, _ in transfers], local_sem=T.sem[lsem])
        sent[lsem] = sent.get(lsem, 0) + sum(n for _, n in transfers)

    def push(ap, rsem, lsem, deps, dsts=None, lane="a", more=()):
        call(list(more) + [transfer(ids, dsts or [ap] * len(peers), ap, rsem, lane)], lsem, deps)
        came[rsem] = (rsem, len(LANES[lane]) * len(peers))

    PB = [T["bank%d" % i] for i in range(8)]
    eye = T.rep[:, 0:128]

    dm = load("y", T.mc[:], T.mu[:], "ldm")
    dxl = load("s", T.dx[:, 64:128], T.x[:], "ldx")
    da = load("y", T.angi[:], T.ang[:], "lda")
    dc = load("y", T.cnt[:], T.counts[:], "ldc")
    ones = op("v", ms(eye, 1.0))
    c_eye = op("q", lambda e: e.affine_select(eye, eye, [[-1, 128]], A.is_equal, 0.0, 0, 1), [ones])
    c_p = op("q", lambda e: e.iota(T.ip[:], [[0, 1]], 0, 1))
    c_a = op("q", lambda e: e.iota(T.a64[:], [[2, 64]], -63, 0, allow_small_or_imprecise_dtypes=True))
    c_b = op("q", lambda e: e.iota(T.b4i[:], [[32, 4]], 0, 0, allow_small_or_imprecise_dtypes=True))
    tails = [op("v", ms(T.D[:, 4096:4104], 1.0))]
    for b in (T.X, T.W, T.f):
        tails.append(op("v", ms(b[:, 4096:4104], 0.0)))
    c_0 = op("v", ms(T.zer[:], 0.0))
    c_rep = [c_eye]
    for j in range(1, 8):
        o = T.rep[:, 128 * j:128 * j + 128]
        c_rep.append(op("v", cp(o, eye), [c_eye]) if j < 5 else op("s", act(o, eye), [c_eye]))

    def slot(buf, j):
        return buf[:, 64 * (j - 1):64 * j]

    if XP:
        send(partner, T.pdx[:, 64:128], T.dx[:, 64:128], "cx", [dxl])
    else:
        push(T.dx[:, 64:128], "cy", "lr", [dxl], [slot(T.fx, j) for j in range(1, NQ)], "h")

    def blk(win, q, h0=0, h1=512):
        return win[:, 512 * q + h0:512 * q + h1]

    def spread(src, h0, h1, bank, deps):
        return (h0, h1, bank, [op("p", mm(PB[bank][:, 64 * (h - h0):64 * (h - h0) + 64], T.rep[:, h:1024:8], src, True, True),
                                  c_rep + list(deps), bank) for h in range(h0, h1)][-1])

    def settle(eng, win, q, m):
        h0, h1, bank, d = m
        o, f = blk(win, q, 64 * h0, 64 * h1), PB[bank][:, 0:64 * (h1 - h0)]
        return op(eng, cp(o, f) if eng == "v" else act(o, f), [d], bank)

    m_x = spread(T.dx[:, 64:128], 0, 8, 0, [dxl])

    sq = [T.sq[:, 64 * i:64 * i + 64] for i in range(3)]
    rq = [T.rq[:, 64 * i:64 * i + 64] for i in range(5)]
    ss = [op("s", lambda e: e.activation(sq[i], T.mc[:], AF.Square, bias=QUAD[i][0]), [dm]) for i in range(3)]
    r0 = op("v", ts(rq[0], sq[0], QUAD[0][1], A.add, -KQ, A.mult), [ss[0]])
    r1 = op("v", ts(rq[1], sq[1], QUAD[1][1], A.add), [ss[1]])
    r2 = op("v", ts(rq[2], sq[2], QUAD[2][1], A.add), [ss[2]])
    r0 = op("v", tt(rq[3], rq[0], T.mc[:], A.mult), [r0])
    r3 = op("v", tt(rq[4], rq[1], rq[2], A.mult), [r1, r2])
    r4 = op("v", tt(sq[0], rq[4], rq[3], A.mult), [r0, r3])
    d_c = op("v", ts(T.dx[:, 0:64], sq[0], 1.0, A.add), [r4])
    send(partner, T.pdx[:, 0:64], T.dx[:, 0:64], "cd", [d_c])
    if not XP:
        send(partner, T.pdx[:, 64:128], T.dx[:, 64:128], "cx", [dxl])
    c_z = op("q", lambda e: e.iota(T.ipz[:], [[-1, 16]], 0, 1))
    ev = [settle("s", T.X, rank, m_x)]
    m_d = [spread(T.dx[:, 0:64], 0, 4, 1, [d_c]), spread(T.dx[:, 0:64], 4, 8, 2, [d_c])]

    a0 = op("v", cp(T.angf[:, 0:2], T.angi[:]), [da])
    a1 = op("v", ts(T.ip2[:], T.ip[:], 15, A.bitwise_and), [c_p])
    a2 = op("v", ts(T.angf[:, 2:3], T.angf[:, 1:2], -1.0, A.mult), [a0])
    a3 = op("v", ts(T.fm[:], T.ip2[:], 2.0, A.mult, -63.0, A.add), [a1])
    a4 = op("v", ts(T.b4[:], T.b4i[:], T.fm[:, 0:1], A.add), [a3, c_b])
    a5 = op("v", ts(T.kc[:], T.b4[:], T.angf[:, 2:3], A.mult, 16384.0, A.add), [a4, a2])
    a6 = op("v", ts(T.kr[:], T.b4[:], T.angf[:, 0:1], A.mult, 16384.0, A.add), [a4])
    e_d = [settle("v", T.D, rank, m_d[0]), settle("s", T.D, rank, m_d[1])]
    push(blk(T.D, rank), "pd0", "ld0", e_d)

    def before(j, s):
        return members[s][(me - j) % NQ]

    widths = sorted({(hi - lo) // 8 for _, lo, hi in STAGES})
    rat = {w: sum(widths[:n]) // 2 for n, w in enumerate(widths)}
    c_r = [op("q", lambda e: e.iota(T.rli[:, rat[w]:rat[w] + w // 2], [[0, 8], [16, w // 16]], 0, 0,
                                    allow_small_or_imprecise_dtypes=True)) for w in widths]
    nr = sum(widths) // 2
    for k in range(4):
        lc = op("v", ts(T.vc[:, k:256:4], T.a64[:], T.angf[:, 0:1], A.mult, T.kc[:, k:k + 1], A.add), [a5, c_a])
        lr = op("v", ts(T.vr[:, k:256:4], T.a64[:], T.angf[:, 1:2], A.mult, T.kr[:, k:k + 1], A.add), [a6, c_a])
    c1 = op("v", ts(T.col[:], T.vc[:], 9, A.logical_shift_right), [lc])
    c2 = op("v", ts(T.row[:], T.vr[:], 3, A.logical_shift_right, 0x1FFFFFC0, A.bitwise_and), [lr])
    c3 = op("v", ts(T.pen[:], T.col[:], 64.0, A.is_ge, 4096.0, A.mult), [c1])
    c4 = op("v", tt(T.raw[:], T.col[:], T.row[:], A.add), [c1, c2])
    c6 = op("v", tt(T.raw2[:], T.raw[:], T.pen[:], A.add), [c3, c4])
    fl = op("v", ts(T.fl[:], T.raw2[:], 4096.0, A.min), [c6])
    cd = ("cd", ne_off)
    if DP < 8:
        push(T.pdx[:, 0:64], "fd", "lr", [cd], [slot(T.fd, j) for j in range(1, NQ)])
    arrived = ["pw1", "pw0"] if XP else ["pw1"]
    banks = [3]

    def setup(steps):
        for step in steps.split():
            banks[0] = (banks[0] + 1) % 8
            what, eng, b = step[0:2], step[2], banks[0]
            if what == "da":
                e_d.append(settle(eng, T.D, partner, spread(T.pdx[:, 0:64], 0, DP, b, [cd])))
                push(blk(T.D, partner, 0, 64 * DP), "pd1", "ld1", e_d[-1:])
                if XP and not XF:
                    push(blk(T.X, rank), "pw0", "lw0", ev)
            elif what == "db":
                e_d.append(settle(eng, T.D, partner, spread(T.pdx[:, 0:64], DP, 8, b, [cd])))
            elif what == "xp":
                ev.append(settle(eng, T.X, partner, spread(T.pdx[:, 64:128], 0, 8, b, [("cx", ne_off)])))
                xp = ev[-1]
            elif what == "xw":
                if XF:
                    push(blk(T.X, partner), "pw1", "lw1", ev, None, "h",
                         [transfer(ids, [blk(T.X, rank)] * len(peers), blk(T.X, rank), "pw1", "l")])
                    came["pw0"] = came["pw1"] = ("pw1", npush)
                else:
                    push(blk(T.X, partner), "pw1", "lw1", ev)
            elif what[0] == "f":
                j = int(what[1])
                e_d.append(settle(eng, T.D, before(j, 1 - ci), spread(slot(T.fd, j), DP, 8, b, [came["fd"]])))
            else:
                j = int(what[1])
                ev.append(settle(eng, T.X, before(j, ci), spread(slot(T.fx, j), 0, 8, b, [came["cy"]])))

    setup(SETUP[0])
    in0 = op("v", ms(T.ind[:], 0.0))
    in1 = op("v", ms(T.ind[:, 0:1024:64], 1.0), [in0])
    c5 = op("v", ts(T.tp[:], T.vr[:], 9, A.arith_shift_right), [lr])
    s_1 = op("v", ts(T.ipz2[:], T.ipz[:], 15, A.bitwise_and), [c_z])
    s_sel = op("v", ts(T.ssel[:], T.ipz[:], 0.0, A.is_equal, 2048.0, A.mult), [c_z])
    s_sum = op("v", ts(T.ssum[:], T.ipz2[:], 0.0, A.is_equal), [s_1])
    p16 = op("v", cp(T.p16[:], T.ip2[:]), [a1])
    rl = op("v", ts(T.rl[:, 0:nr], T.rli[:, 0:nr], T.p16[:, 0:1], A.add), c_r + [p16])
    RL = {w: T.rl[:, rat[w]:rat[w] + w // 2] for w in widths}

    def theirs(j, s):
        return members[s][(me + j) % NQ]

    def wsrc(j, s, lo, hi):
        return blk(T.wb, s, lo, hi) if j == 0 else blk(T.wl, 2 * (j - 1) + s, lo, hi)

    def rays(j, s, lo, hi):
        t, b = (T.tl, s) if j == 0 else (T.tll, 2 * (j - 1) + s)
        return t[:, 32 * b + lo // 16:32 * b + hi // 16]

    for j in range(NQ):
        for s in range(2):
            o, b = 64 * j + 32 * s, 32 * theirs(j, s)
            tl = op("v", ts(T.tl[:, o:o + 32], T.tp[:, b:b + 32], 0.0, A.max, 63.0, A.min), [c5])
    call([transfer([ids[j - 1]], [T.tll[:, 64 * j - 64:64 * j]], T.tl[:, 64 * j:64 * j + 64], "tx", j) for j in range(1, NQ)],
         "lr", [tl])
    tx = ("tx", sum(len(LANES[j]) for j in range(1, NQ)))

    def gath(eng, out, win, off, deps):
        src = win.indirect(off)
        return op(eng, cp(out, src) if eng == "v" else act(out, src), deps)

    setup(SETUP[1])
    for eng in ("s", "v"):
        wait(eng, "pd0", npush)
        wait(eng, "pd1", npush)

    dg = {a: gath(eng, T.f[:, 64 * a:64 * z], T.D[:], T.fl[:, 4 * a:4 * z], [fl] + e_d + tails) for eng, a, z in DCH}
    wsc = []
    for n, (eng, a, z) in enumerate(DCH):
        wsc.append(op("v", scan(T.W[:, 64 * a:64 * z], T.ind[:, 0:64 * (z - a)], T.f[:, 64 * a:64 * z], A.max, A.mult),
                      [dg[a], in1]))
        if n == 0:
            setup(SETUP[2])
    d0 = op("v", cp(T.d0[:], T.f[:, 0:4096:64]), wsc)
    fz = op("v", ms(T.f[:, 0:4096:64], 0.0), [d0])

    def xgath(eng, a, z):
        return (a, z, gath(eng, T.xg[:, 64 * a:64 * z], T.X[:], T.fl[:, 4 * a:4 * z], [fl] + ev + tails))

    def hscan(a, z, dep):
        lo = 64 * a - 1 if a else None
        return op("v", scan(T.st[:, 64 * z - 1:lo:-1], T.f[:, 64 * z:64 * a:-1], T.xg[:, 64 * z - 1:lo:-1]), [dep, fz])

    have, loc = {}, {}

    def wgath(eng, j, s):
        b = theirs(j, s)
        d = have[(j, s)] = gath(eng, blk(T.wb, 2 * j + s), T.W[:], T.fl[:, 32 * b:32 * b + 32], wsc + tails)
        if j in WPAIR:
            if (j, 1 - s) in have:
                send(peers[j - 1], T.wl[:, 1024 * j - 1024:1024 * j], T.wb[:, 1024 * j:1024 * j + 1024], "wx_%d_0" % j,
                     [d, have[(j, 1 - s)]])
                have[(j, 0)] = have[(j, 1)] = ("wx_%d_0" % j, ne_on)
        elif j:
            send(peers[j - 1], wsrc(j, s, 0, 512), blk(T.wb, 2 * j + s), "wx_%d_%d" % (j, s), [d])
            have[(j, s)] = ("wx_%d_%d" % (j, s), ne_on)

    def place(c):
        b = 3 + PLACED.index(c)
        loc[c] = op("p", mm(PB[b][:], eye, wsrc(c[0], c[1], 0, 512), True, True), [have[c]], b)

    for k in range(R):
        last = k == R - 1
        stages = [(s, lo, hi) for s in (1 - ci, ci) for lo, hi in CUTL] if last else STAGES
        NS = len(stages)
        wid = [(h - l) // 8 for _, l, h in stages]
        off = [sum(wid[:i]) for i in range(NS)]
        for eng in ("s", "v") if k else ():
            waits(eng, [came[n] for n in arrived])

        def addin(i, buf, at, sel, deps, stop=False, early=False):
            s, lo, hi = stages[i]
            nb = (hi - lo) // 128
            o = wid[i - 3] if early and i >= 3 else 0
            return [op("p", mm(PB[i % 3][:, o + b:o + 16 * nb:nb], buf[:, at + lo + 128 * b:at + lo + 128 * b + 128], sel, False,
                               stop and b == nb - 1), deps, i % 3) for b in range(nb)][-1]

        both = [wid[i] + (wid[i + 3] if i + 3 < NS else 0) for i in range(NS)]
        zs = [op("p", mm(PB[i][:, 0:both[i]], eye, T.zer[:, 0:both[i]], True, False), [c_0, c_eye], i) for i in range(3)]
        for i in range(NS):
            addin(i, T.X, 512 * theirs(0, stages[i][0]), T.ssel[:], [zs[i % 3], s_sel] + ev, early=True)
        if k == 0:
            for n, c in enumerate(WV):
                wgath("s" if n in WS0 else "v", *c)
            waits("s", [came[n] for n in arrived])
            sc = [xgath("s", a, z) for a, z in XCH0]
            for c in WS:
                wgath("s", *c)
            hs = [hscan(*c) for c in sc]
            for c in PLACE0:
                place(c)
        else:
            sc = [xgath("s", a, z) for a, z in zip(XS, XS[1:])]
            hs = []
            for c in XV:
                hs.append(hscan(*(xgath("v", *c) if c else sc.pop(0))))

        def ewin(j):
            return T.el[:, 256 * k + 64 * j:256 * k + 64 * j + 64]

        e0 = op("v", tt(T.u[:], T.d0[:], T.st[:, 0:4096:64], A.mult), hs + [d0])
        ee = op("v", tt(ewin(0), T.cnt[:], T.u[:], A.subtract), [e0, dc])
        if ESPLIT:
            for j in range(1, NQ):
                send(peers[j - 1], ewin(j), ewin(0), "ex_%d_%d" % (k, j), [ee])
            ex = {j: ("ex_%d_%d" % (k, j), ne_on) for j in range(1, NQ)}
        else:
            push(ewin(0), "ex_%d_1" % k, "lr", [ee], [ewin(j) for j in range(1, NQ)])
            ex = {j: ("ex_%d_1" % k, npush) for j in range(1, NQ)}

        def egath(j, s, lo, hi):
            at = 1024 * j + 512 * s
            deps = [ee, tl] if j == 0 else [ex[j], tx]
            return gath("s", T.eg[:, at + lo:at + hi], ewin(j), rays(j, s, lo, hi), deps)

        def mult(j, s, lo, hi, got):
            at = 1024 * j + 512 * s
            out = T.pr[:, at + lo:at + hi]
            if got is None:
                deps = [ee, tl] if j == 0 else [ex[j], tx]
                return op("v", tt(out, ewin(j).indirect(rays(j, s, lo, hi)), wsrc(j, s, lo, hi), A.mult), deps + [have[(j, s)]])
            b = 3 + PLACED.index((j, s))
            return op("v", tt(out, T.eg[:, at + lo:at + hi], PB[b][:, lo:hi], A.mult), [got, loc[(j, s)]], b)

        got, own, full, pts, reps, turned, news, evs = {}, {}, {}, {}, {}, {}, {}, []

        def relu(eng, out, in_, deps, bank):
            return op(eng, ts(out, in_, STEP, A.mult, 0.0, A.max) if eng == "v" else act(out, in_, AF.Relu, STEP), deps, bank)

        for step in (BACK0 if k == 0 else LAST if last else BACK).split():
            what, i = step[0], int(step[1])
            if what == "w":
                wgath(step[3], i, int(step[2]))
                continue
            if what == "p":
                place((i, int(step[2])))
                continue
            if what == "G":
                got[(0, i)] = egath(0, i, 0, 512)
                continue
            if what == "M":
                own[i] = mult(0, i, 0, 512, got.get((0, i)))
                for n in range(NS):
                    if stages[n][0] == i:
                        addin(n, T.pr, 512 * i, T.ssum[:], [own[i], s_sum], early=True)
                continue
            s, lo, hi = stages[i]
            w, m, r, p, nb = wid[i], 128 * k + off[i], 8 * off[i], 512 * theirs(0, s) + lo, (hi - lo) // 128
            mp = 256 * k + sum(both[:i])
            acc, bank = PB[i % 3][:, 0:w], (TURNL if last else TURN)[i]
            if what == "g":
                got[step[1:]] = egath(int(step[2]), s, lo, hi)
            elif what == "m":
                j = int(step[2])
                pd = mult(j, s, lo, hi, got.get(step[1:]))
                full[i] = addin(i, T.pr, 1024 * j + 512 * s, T.ssum[:], [pd], j == NQ - 1)
            elif what == "o":
                at = 256 * k + sum(both[:i - 3]) + wid[i - 3]
                wait("p", *op("p", mm(acc, eye, T.pt[:, at:at + w], True, False), [pts[i - 3]], i % 3))
            elif what == "l":
                o, f = T.pt[:, mp:mp + both[i]], PB[i % 3][:, 0:both[i]]
                pts[i] = op(step[2], cp(o, f) if step[2] == "v" else act(o, f), [full[i]], i % 3)
                held = (T.xs[:, m:m + w], T.pt[:, mp:mp + w], "xc_%d_%d" % (k, i), [pts[i]])
                if len(step) == 3:
                    send(partner, *held)
            elif what == "r":
                reps[i] = gath(step[2], T.ptr[:, r:r + 8 * w], T.pt[:, mp:mp + w], RL[w], [pts[i], rl, hist.get("n")])
            elif what == "a":
                n = hist["n"] = op("v", tt(T.rp[:, r:r + 8 * w], T.xs[:, m:m + w].indirect(RL[w]), T.ptr[:, r:r + 8 * w], A.add),
                                   [reps[i], ("xc_%d_%d" % (k, i), ne_off), hist.get(i)])
                hist[i] = turned[i] = [op("p", mm(PB[bank][:, 128 * b:128 * b + 128], T.rp[:, r + b:r + 8 * w:nb], eye, True, True),
                                          [n], bank) for b in range(nb)][-1]
            elif what == "x":
                left = "lp_%d_%d" % (k - 1, i) if k else "lw%d" % (s != ci or XF)
                wait(step[2], left, sent.get(left, 0))
                d = relu(step[2], T.X[:, p:p + hi - lo], PB[bank][:, 0:hi - lo], [turned[i]], bank)
                push(T.X[:, p:p + hi - lo], "pu_%d_%d" % (k, i), "lp_%d_%d" % (k, i), [d], lane=step[3])
                evs.append(d)
            elif what == "c":
                def nn(j, at=512 * k + off[i], w=w):
                    return T.nn[:, at + 128 * j:at + 128 * j + w]
                news[i] = nn
                d = reps[i] = op("v", tt(nn(0), T.pt[:, mp:mp + w], T.xs[:, m:m + w], A.add), [pts[i], ("xc_%d_%d" % (k, i), ne_off)])
                if step[2] == "b":
                    two = [T.nn[:, 512 * k + 128 * j + off[i - 1]:512 * k + 128 * j + off[i] + w] for j in range(NQ)]
                    push(two[0], "pu_%d_%d" % (k, i), "lr", [d], two[1:])
                    came["pu_%d_%d" % (k, i - 1)] = came["pu_%d_%d" % (k, i)]
                elif step[2] == "f":
                    push(nn(0), "pu_%d_%d" % (k, i), "lr", [d] + held[3], [nn(j) for j in range(1, NQ)], "h",
                         [transfer([other], [held[0]], held[1], held[2], "l")])
                elif step[2] == "a":
                    push(nn(0), "pu_%d_%d" % (k, i), "lr", [d], [nn(j) for j in range(1, NQ)])
            elif what == "e":
                j = int(step[2])
                at = 4 * r + 8 * w * j
                reps[(i, j)] = gath(step[3], T.rp4[:, at:at + 8 * w], news[i](j), RL[w],
                                    [rl, came["pu_%d_%d" % (k, i)] if j else reps[i], hist.get((i, j))])
            if what == "t" or what == "e" and len(step) == 5:
                j, bank = int(step[2]), int(step[-1])
                at = 4 * r + 8 * w * j
                hist[(i, j)] = [op("p", mm(PB[bank][:, 128 * b:128 * b + 128], T.rp4[:, at + b:at + 8 * w:nb], eye, True, True),
                                   [reps[(i, j)]], bank) for b in range(nb)][-1]
                turned[(i, j)] = bank
            elif what == "z":
                j = int(step[2])
                bank, p = turned[(i, j)], 512 * theirs(-j, s) + lo
                if k == 0 and j == 0:
                    wait(step[3], "lw%d" % (s != ci or XF), sent.get("lw%d" % (s != ci or XF), 0))
                evs.append(relu(step[3], T.X[:, p:p + hi - lo], PB[bank][:, 0:hi - lo], [hist[(i, j)]], bank))
            elif what == "n":
                h = i - NS // 2
                mo = 128 * k + off[h]
                n = op("v", tt(T.rp[:, off[h]:off[h] + w], T.xs[:, mo:mo + w], acc, A.add),
                       [full[i], ("xc_%d_%d" % (k, h), ne_off), hist.get(0)], i % 3)
                tp = [op("p", mm(PB[bank][0:16, 128 * b:128 * b + 128], T.rp[:, off[h] + b:off[h] + w:nb], eye, True, True),
                         [n], bank) for b in range(nb)][-1]
                turned[i] = tp
            elif what == "y":
                evs.append(relu(step[2], T.ysb[0:16, lo:hi], PB[bank][0:16, 0:hi - lo], [turned[i]], bank))
        if last:
            waits("y", evs)
            load("y", T.y[:], T.ysb[0:16, :], "yo")
        ev = evs
        arrived = ["pu_%d_%d" % (k, i) for i in range(NS)]

    for e in ("v", "s", "p", "q"):
        wait("q", e, cnt[e])
    for n in sorted(sent):
        wait("q", n, sent[n])
    for n in ("ldm", "ldx", "lda", "ldc", "yo"):
        wait("q", n, hist[n])
